import numpy as np
import ml_dtypes


def mxq(x, axis, fmt="e4m3"):
    dtype, down = {"e4m3": (ml_dtypes.float8_e4m3fn, 7), "e5m2": (ml_dtypes.float8_e5m2, 14)}[fmt]
    v = np.moveaxis(np.asarray(x, np.float32).astype(ml_dtypes.bfloat16).astype(np.float64), axis, -1)
    blocks = v.reshape(v.shape[:-1] + (-1, 32))
    amax = np.abs(blocks).max(-1, keepdims=True)
    byte = np.maximum(np.where(amax > 0, np.frexp(amax)[1] - 1 + 127, 0) - down, 1)
    scale = np.exp2(byte - 127.0)
    codes = (blocks / scale).astype(np.float32).astype(dtype).astype(np.float64)
    return np.moveaxis((codes * scale).reshape(v.shape), -1, axis)


WIDE = False


def mx_kscale(k):
    if not WIDE:
        return np.ones(k)
    levels = np.array([10, -10, 5, -5, 0])
    if k % 512:
        return np.exp2(np.random.permutation(np.resize(levels, k // 32))).repeat(32)
    a = np.empty((k // 512, 16))
    for p in range(k // 512):
        a[p, :8] = np.random.permutation(np.resize(levels, 8))
        for g in range(8):
            far = levels[np.abs(levels - a[p, g]) >= 10]
            a[p, g + 8] = far[np.random.randint(len(far))]
    return np.exp2(a.ravel()).repeat(32)


def f64(x):
    return np.asarray(x).astype(np.float64)


def striped(idx):
    return np.tile(idx.reshape(-1, 16).T, (8, 1)).astype(np.uint16)


def unstriped(offs):
    return offs[:16].T.reshape(-1).astype(np.int64)


def pack_weight(w):
    k, n = w.shape
    w = f64(np.asarray(w, np.float32).astype(ml_dtypes.bfloat16)).reshape(k // 32, 32, n)
    amax = np.abs(w).max(1)
    byte = np.clip(np.where(amax > 0, np.frexp(amax)[1] - 1 + 127 - 7, 1), 1, 254)
    scaled = (w * np.exp2(127.0 - byte)[:, None, :]).reshape(k, n).astype(np.float32)
    words = np.ascontiguousarray(scaled.reshape(k // 512, 128, 4, n).transpose(0, 1, 3, 2)).astype(ml_dtypes.float8_e4m3fn).view(np.uint8)
    return words, np.ascontiguousarray(byte.astype(np.uint8).reshape(k // 512, 16, n))


def unpack_weight(words, scales):
    g, p, n, _ = words.shape
    vals = np.ascontiguousarray(words).view(ml_dtypes.float8_e4m3fn).astype(np.float64) * np.repeat(np.exp2(scales.astype(np.float64) - 127.0), 8, axis=1)[..., None]
    return vals.transpose(0, 1, 3, 2).reshape(g * 512, n)


def planes(y):
    n, m = y.shape
    v = y.astype(np.float32).astype(ml_dtypes.bfloat16).astype(np.float64).reshape(n // 32, 32, m)
    top = np.abs(v).max(1)
    byte = np.clip(np.where(top > 0, np.frexp(top)[1] - 1 + 127 - 7, 1), 1, 254)
    codes = (v * np.exp2(127.0 - byte)[:, None, :]).reshape(n, m).astype(np.float32).astype(ml_dtypes.float8_e4m3fn).view(np.uint8)
    words = codes.reshape(n // 512, 128, 4, m).transpose(0, 1, 3, 2)
    return np.ascontiguousarray(words), np.ascontiguousarray(byte.astype(np.uint8).reshape(n // 512, 16, m))


K, T, S, D, V, H, N = 512, 4096, 1024, 4, 256, 512, 512
P = 2 ** 7


def setup_inputs():
    n = np.random.standard_normal
    s = mx_kscale(K)[:, None]
    u = mx_kscale(H)
    packed_xT = pack_weight(n((K, T)) * s)
    return {
        "x_words": packed_xT[0],
        "x_scales": packed_xT[1],
        "w1": (n((K, H)) / np.sqrt(K) / s * u).astype(np.float32),
        "w2": (n((H, N)) / np.sqrt(H) / u[:, None]).astype(np.float32),
        "gate": (np.tile(np.random.uniform(0.2, 1.0, (D, 1, V)), (1, P, 1))).astype(np.float32),
        "offs": striped(np.random.permutation(T)[:S]),
    }


def reference(x_words, x_scales, w1, w2, gate, offs):
    xq = unpack_weight(x_words, x_scales)[:, unstriped(offs)]
    w1q = mxq(f64(w1), 0, "e4m3")
    y0 = w1q.T @ xq[:, :V]
    y1 = w1q.T @ xq[:, V:2 * V]
    y2 = w1q.T @ xq[:, 2 * V:3 * V]
    y3 = w1q.T @ xq[:, 3 * V:4 * V]
    z = y0 * f64(gate)[0, :1] + y1 * f64(gate)[1, :1] + y2 * f64(gate)[2, :1] + y3 * f64(gate)[3, :1]
    out_0 = mxq(f64(w2), 0, "e4m3").T @ mxq(z, 0, "e4m3")
    return (out_0,) + planes(out_0)

@@ -1,0 +1,173 @@
+from contextlib import ExitStack
+
+import concourse.mybir as mybir
+from concourse.masks import make_identity
+
+K, T, S, D, V, H, N = 512, 4096, 1024, 4, 256, 512, 512
+P = 128
+PACK = 4
+HALVES = V // P
+
+FLOPS = 2 * K * H * S + 2 * H * N * V
+BYTES = P * T * PACK + 16 * T + 4 * K * H + 4 * H * N + 4 * D * V + 2 * P * S // 16 + 4 * N * V + N * V + 16 * V
+
+F32 = mybir.dt.float32
+BF16 = mybir.dt.bfloat16
+I32 = mybir.dt.int32
+U32 = mybir.dt.uint32
+U16 = mybir.dt.uint16
+U8 = mybir.dt.uint8
+FP8X4 = mybir.dt.float8_e4m3fn_x4
+MULT = mybir.AluOpType.mult
+ADD = mybir.AluOpType.add
+COPY = mybir.ActivationFunctionType.Copy
+
+
+def tile_picked_zbloom_none_po_kernel(
+    tc, x_words, x_scales, w1, w2, gate, offs, out_0, out_1, out_2
+):
+    nc = tc.nc
+    with ExitStack() as ctx:
+        sb = ctx.enter_context(tc.tile_pool(name="sb", bufs=1))
+        ps = ctx.enter_context(tc.psum_pool(name="ps", bufs=1))
+
+        def bank(b, shape, name):
+            return ps.tile(shape, F32, name=name, tag="bank%d" % b)
+
+        w1_raw = sb.tile([P, PACK, H], F32, name="w1_raw", align_bytes=64)
+        nc.sync.dma_start(out=w1_raw[:], in_=w1.rearrange("(p j) c -> p j c", j=PACK))
+        offsets = sb.tile([P, S // 16], U16, name="offsets")
+        nc.sync.dma_start(offsets[:], offs)
+
+        scale_table = sb.tile([P, T], U8, name="scale_table", align_bytes=64)
+        nc.vector.memset(scale_table[:].bitcast(I32), 0)
+        for q in range(4):
+            nc.scalar.dma_start(
+                out=scale_table[32 * q : 32 * q + 4, :].bitcast(I32),
+                in_=x_scales[0, 4 * q : 4 * q + 4, :].bitcast(I32),
+            )
+        gate_rows = sb.tile([P, V], F32, name="gate_rows", align_bytes=64)
+        nc.gpsimd.memset(gate_rows[:], 0.0)
+        nc.scalar.dma_start(out=gate_rows[0:D, :], in_=gate[:, 0, :])
+
+        word_table = sb.tile([P, T], U32, name="word_table", align_bytes=64)
+        nc.sync.dma_start(
+            out=word_table[:].bitcast(I32),
+            in_=x_words[0].rearrange("p n t -> p (n t)").bitcast(I32),
+        )
+        w2_view = w2.rearrange("(p j) c -> p j c", j=PACK)
+        w2_raw = []
+        for a in range(2):
+            part = sb.tile([P, PACK, N // 2], F32, name="w2_raw%d" % a, align_bytes=64)
+            nc.sync.dma_start(out=part[:], in_=w2_view[:, :, a * (N // 2) : (a + 1) * (N // 2)])
+            w2_raw.append(part)
+
+        ident = sb.tile([P, P], F32, name="ident", align_bytes=64)
+        make_identity(nc, ident[:])
+
+        gate_ps = bank(7, [P, HALVES, P], "gate_ps")
+        for h in range(HALVES):
+            nc.tensor.transpose(gate_ps[:, h, :], gate_rows[:, h * P : (h + 1) * P], ident[:])
+        gate_col = sb.tile([P, HALVES, D], F32, name="gate_col", align_bytes=64)
+        nc.scalar.activation(gate_col[:], gate_ps[:, :, 0:D], COPY)
+
+        w1_bf = sb.tile([P, H * PACK], BF16, name="w1_bf", align_bytes=64)
+        nc.scalar.copy(
+            out=w1_bf[:].rearrange("p (u q e j) -> p q u e j", u=2, e=2, j=PACK),
+            in_=w1_raw[:].rearrange("p j (q u e) -> p q u e j", u=2, e=2),
+        )
+        w1_codes = sb.tile([P, H], U32, name="w1_codes", align_bytes=64)
+        w1_scales = sb.tile([P, H], U8, name="w1_scales", align_bytes=64)
+        nc.vector.quantize_mx(out=w1_codes[:].bitcast(FP8X4), scales=w1_scales[:], in_=w1_bf[:])
+
+        x_sc = sb.tile([P, S], U8, name="x_sc", align_bytes=64)
+        nc.vector.tensor_copy(x_sc[:], scale_table[:].indirect(offsets[:]))
+        x_w = []
+        for a in range(2):
+            part = sb.tile([P, S // 2], U32, name="x_w%d" % a, align_bytes=64)
+            nc.vector.tensor_copy(part[:], word_table[:].indirect(offsets[:, a * 32 : (a + 1) * 32]))
+            x_w.append(part)
+
+        y = {}
+        for h in range(HALVES):
+            for d in range(D):
+                y[h, d] = bank(h * D + d, [P, H], "y%d%d" % (h, d))
+                first = d * V + h * P
+                local = first % (S // 2)
+                nc.tensor.matmul_mx(
+                    out=y[h, d][:],
+                    lhsT=x_w[d // 2][:, local : local + P].bitcast(FP8X4),
+                    lhsT_scale=x_sc[:, first : first + P],
+                    rhs=w1_codes[:].bitcast(FP8X4),
+                    rhs_scale=w1_scales[:],
+                    start=True,
+                    stop=True,
+                )
+
+        z_codes = sb.tile([P, V], U32, name="z_codes", align_bytes=64)
+        z_scales = sb.tile([P, V], U8, name="z_scales", align_bytes=64)
+        z_bf = []
+        for h in range(HALVES):
+            acc = sb.tile([P, H], F32, name="acc%d0" % h, align_bytes=64)
+            nc.scalar.activation(acc[:], y[h, 0][:], COPY, scale=gate_col[:, h, 0:1])
+            for d in range(1, D):
+                nxt = sb.tile([P, H], BF16 if d == D - 1 else F32, name="acc%d%d" % (h, d), align_bytes=64)
+                nc.vector.scalar_tensor_tensor(nxt[:], y[h, d][:], gate_col[:, h, d : d + 1], acc[:], MULT, ADD)
+                acc = nxt
+            z_ps = bank(h * D, [P, 2, P], "z_ps%d" % h)
+            pairs = acc[:].bitcast(F32)
+            for u in range(2):
+                nc.tensor.transpose(z_ps[:, u, :], pairs[:, u * P : (u + 1) * P], ident[:])
+            grouped = sb.tile([P, P * PACK], BF16, name="z_bf%d" % h, align_bytes=64)
+            nc.scalar.copy(
+                out=grouped[:].bitcast(F32).rearrange("p (v u) -> p v u", u=2),
+                in_=z_ps[:].rearrange("p u v -> p v u"),
+            )
+            z_bf.append(grouped)
+
+        w2_bf = sb.tile([P, N * PACK], BF16, name="w2_bf", align_bytes=64)
+        w2_dst = w2_bf[:].rearrange("p (t m j) -> p m t j", t=PACK, j=PACK)
+        for a in range(4):
+            src = w2_raw[a // 2][:, :, (a % 2) * P : (a % 2 + 1) * P]
+            nc.scalar.copy(
+                out=w2_dst[:, a * 32 : (a + 1) * 32, :, :],
+                in_=src.rearrange("p j (m t) -> p m t j", t=PACK),
+            )
+        w2_codes = sb.tile([P, N], U32, name="w2_codes", align_bytes=64)
+        w2_scales = sb.tile([P, N], U8, name="w2_scales", align_bytes=64)
+        nc.vector.quantize_mx(out=w2_codes[:].bitcast(FP8X4), scales=w2_scales[:], in_=w2_bf[:])
+
+        out_codes = sb.tile([P, V], U32, name="out_codes", align_bytes=64)
+        out_scales = sb.tile([P, V], U8, name="out_scales", align_bytes=64)
+        out_view = out_0.rearrange("(p t) v -> p t v", t=PACK)
+        words_view = out_1[0].rearrange("p n t -> p (n t)").bitcast(I32)
+        for h in range(HALVES):
+            cols = slice(h * P, (h + 1) * P)
+            nc.vector.quantize_mx(out=z_codes[:, cols].bitcast(FP8X4), scales=z_scales[:, cols], in_=z_bf[h][:])
+            o_ps = bank(h * D + 1, [P, PACK, P], "o_ps%d" % h)
+            for t in range(PACK):
+                nc.tensor.matmul_mx(
+                    out=o_ps[:, t, :],
+                    lhsT=w2_codes[:, t * P : (t + 1) * P].bitcast(FP8X4),
+                    lhsT_scale=w2_scales[:, t * P : (t + 1) * P],
+                    rhs=z_codes[:, cols].bitcast(FP8X4),
+                    rhs_scale=z_scales[:, cols],
+                    start=True,
+                    stop=True,
+                )
+            o_f32 = sb.tile([P, PACK, P], F32, name="o_f32%d" % h, align_bytes=64)
+            nc.scalar.copy(out=o_f32[:], in_=o_ps[:])
+            nc.sync.dma_start(out=out_view[:, :, cols], in_=o_f32[:])
+            o_bf = sb.tile([P, P * PACK], BF16, name="o_bf%d" % h, align_bytes=64)
+            nc.vector.tensor_copy(
+                out=o_bf[:].rearrange("p (v t) -> p v t", t=PACK),
+                in_=o_f32[:].rearrange("p t v -> p v t"),
+            )
+            nc.vector.quantize_mx(out=out_codes[:, cols].bitcast(FP8X4), scales=out_scales[:, cols], in_=o_bf[:])
+            nc.sync.dma_start(out=words_view[:, cols], in_=out_codes[:, cols].bitcast(I32))
+        for q in range(4):
+            queue = nc.sync if q % 2 == 0 else nc.scalar
+            queue.dma_start(
+                out=out_2[0, 4 * q : 4 * q + 4, :].bitcast(I32),
+                in_=out_scales[32 * q : 32 * q + 4, :].bitcast(I32),
+            )

@@ -7,6 +7,7 @@ K, T, S, D, V, H, N = 512, 4096, 1024, 4, 256, 512, 512
 P = 128
 PACK = 4
 HALVES = V // P
+HALF = 256
 
 FLOPS = 2 * K * H * S + 2 * H * N * V
 BYTES = P * T * PACK + 16 * T + 4 * K * H + 4 * H * N + 4 * D * V + 2 * P * S // 16 + 4 * N * V + N * V + 16 * V
@@ -34,36 +35,49 @@ def tile_picked_zbloom_none_po_kernel(
         def bank(b, shape, name):
             return ps.tile(shape, F32, name=name, tag="bank%d" % b)
 
-        w1_raw = sb.tile([P, PACK, H], F32, name="w1_raw", align_bytes=64)
-        nc.sync.dma_start(out=w1_raw[:], in_=w1.rearrange("(p j) c -> p j c", j=PACK))
-        offsets = sb.tile([P, S // 16], U16, name="offsets")
-        nc.sync.dma_start(offsets[:], offs)
-
         scale_table = sb.tile([P, T], U8, name="scale_table", align_bytes=64)
-        nc.vector.memset(scale_table[:].bitcast(I32), 0)
-        for q in range(4):
-            nc.scalar.dma_start(
-                out=scale_table[32 * q : 32 * q + 4, :].bitcast(I32),
-                in_=x_scales[0, 4 * q : 4 * q + 4, :].bitcast(I32),
-            )
+        nc.gpsimd.memset(scale_table[:].bitcast(I32), 0)
         gate_rows = sb.tile([P, V], F32, name="gate_rows", align_bytes=64)
         nc.gpsimd.memset(gate_rows[:], 0.0)
-        nc.scalar.dma_start(out=gate_rows[0:D, :], in_=gate[:, 0, :])
 
+        def load_half(weight, part, name):
+            raw = sb.tile([P, PACK, HALF], F32, name=name, tag=name, align_bytes=64)
+            view = weight.rearrange("(p j) c -> p j c", j=PACK)
+            nc.sync.dma_start(out=raw[:], in_=view[:, :, part * HALF : (part + 1) * HALF])
+            return raw
+
+        w1_raw = [load_half(w1, 0, "w1_raw0")]
+        offsets = sb.tile([P, S // 16], U16, name="offsets")
+        nc.sync.dma_start(offsets[:], offs)
+        for j in range(4):
+            nc.sync.dma_start(
+                out=scale_table[j:P:32, :].bitcast(I32),
+                in_=x_scales[0, j:16:4, :].bitcast(I32),
+            )
+        nc.sync.dma_start(out=gate_rows[0:D, :], in_=gate[:, 0, :])
         word_table = sb.tile([P, T], U32, name="word_table", align_bytes=64)
         nc.sync.dma_start(
             out=word_table[:].bitcast(I32),
             in_=x_words[0].rearrange("p n t -> p (n t)").bitcast(I32),
         )
-        w2_view = w2.rearrange("(p j) c -> p j c", j=PACK)
-        w2_raw = []
-        for a in range(2):
-            part = sb.tile([P, PACK, N // 2], F32, name="w2_raw%d" % a, align_bytes=64)
-            nc.sync.dma_start(out=part[:], in_=w2_view[:, :, a * (N // 2) : (a + 1) * (N // 2)])
-            w2_raw.append(part)
+        w1_raw.append(load_half(w1, 1, "w1_raw1"))
+        w2_raw = [load_half(w2, part, "w2_raw%d" % part) for part in range(2)]
 
         ident = sb.tile([P, P], F32, name="ident", align_bytes=64)
         make_identity(nc, ident[:])
+
+        def quantise_w1(part):
+            rounded = sb.tile([P, HALF * PACK], BF16, name="w1_bf%d" % part, align_bytes=64)
+            nc.scalar.copy(
+                out=rounded[:].rearrange("p (u q e j) -> p q u e j", u=2, e=2, j=PACK),
+                in_=w1_raw[part][:].rearrange("p j (q u e) -> p q u e j", u=2, e=2),
+            )
+            codes = sb.tile([P, HALF], U32, name="w1_codes%d" % part, align_bytes=64)
+            scales = sb.tile([P, HALF], U8, name="w1_scales%d" % part, align_bytes=64)
+            nc.vector.quantize_mx(out=codes[:].bitcast(FP8X4), scales=scales[:], in_=rounded[:])
+            return codes, scales
+
+        w1_mx = [quantise_w1(0)]
 
         gate_ps = bank(7, [P, HALVES, P], "gate_ps")
         for h in range(HALVES):
@@ -71,102 +85,146 @@ def tile_picked_zbloom_none_po_kernel(
         gate_col = sb.tile([P, HALVES, D], F32, name="gate_col", align_bytes=64)
         nc.scalar.activation(gate_col[:], gate_ps[:, :, 0:D], COPY)
 
-        w1_bf = sb.tile([P, H * PACK], BF16, name="w1_bf", align_bytes=64)
-        nc.scalar.copy(
-            out=w1_bf[:].rearrange("p (u q e j) -> p q u e j", u=2, e=2, j=PACK),
-            in_=w1_raw[:].rearrange("p j (q u e) -> p q u e j", u=2, e=2),
-        )
-        w1_codes = sb.tile([P, H], U32, name="w1_codes", align_bytes=64)
-        w1_scales = sb.tile([P, H], U8, name="w1_scales", align_bytes=64)
-        nc.vector.quantize_mx(out=w1_codes[:].bitcast(FP8X4), scales=w1_scales[:], in_=w1_bf[:])
-
         x_sc = sb.tile([P, S], U8, name="x_sc", align_bytes=64)
         nc.vector.tensor_copy(x_sc[:], scale_table[:].indirect(offsets[:]))
         x_w = []
         for a in range(2):
-            part = sb.tile([P, S // 2], U32, name="x_w%d" % a, align_bytes=64)
-            nc.vector.tensor_copy(part[:], word_table[:].indirect(offsets[:, a * 32 : (a + 1) * 32]))
-            x_w.append(part)
+            picked = sb.tile([P, S // 2], U32, name="x_w%d" % a, align_bytes=64)
+            nc.vector.tensor_copy(picked[:], word_table[:].indirect(offsets[:, a * 32 : (a + 1) * 32]))
+            x_w.append(picked)
+        w1_mx.append(quantise_w1(1))
+
+        def first_product(out, d, h, part, lo, hi):
+            codes, scales = w1_mx[part]
+            first = d * V + h * P
+            local = first % (S // 2)
+            nc.tensor.matmul_mx(
+                out=out,
+                lhsT=x_w[d // 2][:, local : local + P].bitcast(FP8X4),
+                lhsT_scale=x_sc[:, first : first + P],
+                rhs=codes[:, lo:hi].bitcast(FP8X4),
+                rhs_scale=scales[:, lo:hi],
+                start=True,
+                stop=True,
+            )
 
         y = {}
+        for d, part in ((0, 0), (1, 0), (2, 0), (0, 1), (1, 1), (2, 1)):
+            y[d, part] = bank(2 * d + part, [P, HALVES, HALF], "y%d%d" % (d, part))
+            for h in range(HALVES):
+                first_product(y[d, part][:, h, :], d, h, part, 0, HALF)
+        y_last = []
         for h in range(HALVES):
-            for d in range(D):
-                y[h, d] = bank(h * D + d, [P, H], "y%d%d" % (h, d))
-                first = d * V + h * P
-                local = first % (S // 2)
-                nc.tensor.matmul_mx(
-                    out=y[h, d][:],
-                    lhsT=x_w[d // 2][:, local : local + P].bitcast(FP8X4),
-                    lhsT_scale=x_sc[:, first : first + P],
-                    rhs=w1_codes[:].bitcast(FP8X4),
-                    rhs_scale=w1_scales[:],
-                    start=True,
-                    stop=True,
+            y_last.append(bank(2 * h, [P, 2, 2, P], "y_last%d" % h))
+            for part in range(2):
+                for u in range(2):
+                    first_product(y_last[h][:, u, part, :], D - 1, h, part, u * P, (u + 1) * P)
+
+        three = [sb.tile([P, 2, 2, P], F32, name="three%d" % h, tag="three%d" % h, align_bytes=64) for h in range(HALVES)]
+        for part in range(2):
+            acc = {}
+            for d in range(D - 1):
+                for h in range(HALVES):
+                    factor = gate_col[:, h, d : d + 1]
+                    name = "acc%d%d%d" % (part, h, d)
+                    if d == D - 2:
+                        nc.vector.scalar_tensor_tensor(
+                            three[h][:, :, part, :],
+                            y[d, part][:, h, :].rearrange("p (u c) -> p u c", u=2),
+                            factor,
+                            acc[h][:].rearrange("p (u c) -> p u c", u=2),
+                            MULT,
+                            ADD,
+                        )
+                        continue
+                    tag = {"acc000": "w1_raw1", "acc101": "acc011"}.get(name, name)
+                    nxt = sb.tile([P, HALF], F32, name=name, tag=tag, align_bytes=64)
+                    if d == 0:
+                        nc.scalar.activation(nxt[:], y[d, part][:, h, :], COPY, scale=factor)
+                    else:
+                        nc.vector.scalar_tensor_tensor(nxt[:], y[d, part][:, h, :], factor, acc[h][:], MULT, ADD)
+                    acc[h] = nxt
+        z_rows = []
+        for h in range(HALVES):
+            z_rows.append(sb.tile([P, H], BF16, name="z_rows%d" % h, align_bytes=64))
+            nc.vector.scalar_tensor_tensor(
+                z_rows[h][:],
+                y_last[h][:].rearrange("p u a c -> p (u a c)"),
+                gate_col[:, h, D - 1 : D],
+                three[h][:].rearrange("p u a c -> p (u a c)"),
+                MULT,
+                ADD,
+            )
+
+        w2_mx = []
+        for pair in range(2):
+            rounded = sb.tile([P, 2, P, PACK], BF16, name="w2_bf%d" % pair, align_bytes=64)
+            for part in range(2):
+                nc.scalar.copy(
+                    out=rounded[:, :, part * 64 : (part + 1) * 64, :].rearrange("p e m j -> p m e j"),
+                    in_=w2_raw[part][:].rearrange("p j (m u e) -> p u m e j", u=2, e=2)[:, pair],
                 )
+            tag = "three1" if pair == 1 else "acc110"
+            codes = sb.tile([P, HALF], U32, name="w2_codes%d" % pair, tag=tag, align_bytes=64)
+            scales = sb.tile([P, HALF], U8, name="w2_scales%d" % pair, align_bytes=64)
+            nc.vector.quantize_mx(
+                out=codes[:].bitcast(FP8X4), scales=scales[:], in_=rounded[:].rearrange("p e m j -> p (e m j)")
+            )
+            w2_mx.append((codes, scales))
 
         z_codes = sb.tile([P, V], U32, name="z_codes", align_bytes=64)
         z_scales = sb.tile([P, V], U8, name="z_scales", align_bytes=64)
-        z_bf = []
         for h in range(HALVES):
-            acc = sb.tile([P, H], F32, name="acc%d0" % h, align_bytes=64)
-            nc.scalar.activation(acc[:], y[h, 0][:], COPY, scale=gate_col[:, h, 0:1])
-            for d in range(1, D):
-                nxt = sb.tile([P, H], BF16 if d == D - 1 else F32, name="acc%d%d" % (h, d), align_bytes=64)
-                nc.vector.scalar_tensor_tensor(nxt[:], y[h, d][:], gate_col[:, h, d : d + 1], acc[:], MULT, ADD)
-                acc = nxt
-            z_ps = bank(h * D, [P, 2, P], "z_ps%d" % h)
-            pairs = acc[:].bitcast(F32)
+            cols = slice(h * P, (h + 1) * P)
+            z_ps = bank(6 + h, [P, 2, P], "z_ps%d" % h)
+            pairs = z_rows[h][:].bitcast(F32)
             for u in range(2):
                 nc.tensor.transpose(z_ps[:, u, :], pairs[:, u * P : (u + 1) * P], ident[:])
-            grouped = sb.tile([P, P * PACK], BF16, name="z_bf%d" % h, align_bytes=64)
+            z_bf = sb.tile([P, P * PACK], BF16, name="z_bf%d" % h, align_bytes=64)
             nc.scalar.copy(
-                out=grouped[:].bitcast(F32).rearrange("p (v u) -> p v u", u=2),
+                out=z_bf[:].bitcast(F32).rearrange("p (v u) -> p v u", u=2),
                 in_=z_ps[:].rearrange("p u v -> p v u"),
             )
-            z_bf.append(grouped)
-
-        w2_bf = sb.tile([P, N * PACK], BF16, name="w2_bf", align_bytes=64)
-        w2_dst = w2_bf[:].rearrange("p (t m j) -> p m t j", t=PACK, j=PACK)
-        for a in range(4):
-            src = w2_raw[a // 2][:, :, (a % 2) * P : (a % 2 + 1) * P]
-            nc.scalar.copy(
-                out=w2_dst[:, a * 32 : (a + 1) * 32, :, :],
-                in_=src.rearrange("p j (m t) -> p m t j", t=PACK),
-            )
-        w2_codes = sb.tile([P, N], U32, name="w2_codes", align_bytes=64)
-        w2_scales = sb.tile([P, N], U8, name="w2_scales", align_bytes=64)
-        nc.vector.quantize_mx(out=w2_codes[:].bitcast(FP8X4), scales=w2_scales[:], in_=w2_bf[:])
+            nc.vector.quantize_mx(out=z_codes[:, cols].bitcast(FP8X4), scales=z_scales[:, cols], in_=z_bf[:])
 
         out_codes = sb.tile([P, V], U32, name="out_codes", align_bytes=64)
         out_scales = sb.tile([P, V], U8, name="out_scales", align_bytes=64)
         out_view = out_0.rearrange("(p t) v -> p t v", t=PACK)
-        words_view = out_1[0].rearrange("p n t -> p (n t)").bitcast(I32)
+        o_ps = []
         for h in range(HALVES):
             cols = slice(h * P, (h + 1) * P)
-            nc.vector.quantize_mx(out=z_codes[:, cols].bitcast(FP8X4), scales=z_scales[:, cols], in_=z_bf[h][:])
-            o_ps = bank(h * D + 1, [P, PACK, P], "o_ps%d" % h)
+            o_ps.append(bank(2 * h + 1, [P, PACK, P], "o_ps%d" % h))
             for t in range(PACK):
                 nc.tensor.matmul_mx(
-                    out=o_ps[:, t, :],
-                    lhsT=w2_codes[:, t * P : (t + 1) * P].bitcast(FP8X4),
-                    lhsT_scale=w2_scales[:, t * P : (t + 1) * P],
+                    out=o_ps[h][:, t, :],
+                    lhsT=w2_mx[t // 2][0][:, t % 2 * P : (t % 2 + 1) * P].bitcast(FP8X4),
+                    lhsT_scale=w2_mx[t // 2][1][:, t % 2 * P : (t % 2 + 1) * P],
                     rhs=z_codes[:, cols].bitcast(FP8X4),
                     rhs_scale=z_scales[:, cols],
                     start=True,
                     stop=True,
                 )
-            o_f32 = sb.tile([P, PACK, P], F32, name="o_f32%d" % h, align_bytes=64)
-            nc.scalar.copy(out=o_f32[:], in_=o_ps[:])
-            nc.sync.dma_start(out=out_view[:, :, cols], in_=o_f32[:])
-            o_bf = sb.tile([P, P * PACK], BF16, name="o_bf%d" % h, align_bytes=64)
-            nc.vector.tensor_copy(
-                out=o_bf[:].rearrange("p (v t) -> p v t", t=PACK),
-                in_=o_f32[:].rearrange("p t v -> p v t"),
+        o_bf = []
+        for h in range(HALVES):
+            o_bf.append(sb.tile([P, P * PACK], BF16, name="o_bf%d" % h, align_bytes=64))
+            round_out = nc.scalar.copy if h == 0 else nc.vector.tensor_copy
+            round_out(
+                out=o_bf[h][:].rearrange("p (v t) -> p v t", t=PACK),
+                in_=o_ps[h][:].rearrange("p t v -> p v t"),
             )
-            nc.vector.quantize_mx(out=out_codes[:, cols].bitcast(FP8X4), scales=out_scales[:, cols], in_=o_bf[:])
-            nc.sync.dma_start(out=words_view[:, cols], in_=out_codes[:, cols].bitcast(I32))
+        for h in range(HALVES):
+            cols = slice(h * P, (h + 1) * P)
+            nc.vector.quantize_mx(out=out_codes[:, cols].bitcast(FP8X4), scales=out_scales[:, cols], in_=o_bf[h][:])
+            o_f32 = sb.tile([P, PACK, P], F32, name="o_f32%d" % h, align_bytes=64)
+            nc.scalar.copy(out=o_f32[:], in_=o_ps[h][:])
+            queue = nc.sync if h == 0 else nc.scalar
+            queue.dma_start(out=out_view[:, :, cols], in_=o_f32[:])
+        nc.sync.dma_start(
+            out=out_1[0].rearrange("p n t -> p (n t)").bitcast(I32),
+            in_=out_codes[:].bitcast(I32),
+        )
         for q in range(4):
-            queue = nc.sync if q % 2 == 0 else nc.scalar
+            queue = nc.sync if q < 2 else nc.scalar
             queue.dma_start(
                 out=out_2[0, 4 * q : 4 * q + 4, :].bitcast(I32),
                 in_=out_scales[32 * q : 32 * q + 4, :].bitcast(I32),

@@ -35,7 +35,7 @@ def tile_picked_zbloom_none_po_kernel(
         def bank(b, shape, name):
             return ps.tile(shape, F32, name=name, tag="bank%d" % b)
 
-        scale_table = sb.tile([P, T], U8, name="scale_table", align_bytes=64)
+        scale_table = sb.tile([P, T], U8, name="scale_table", tag="w2_raw", align_bytes=64)
         nc.gpsimd.memset(scale_table[:].bitcast(I32), 0)
         gate_rows = sb.tile([P, V], F32, name="gate_rows", align_bytes=64)
         nc.gpsimd.memset(gate_rows[:], 0.0)
@@ -49,11 +49,7 @@ def tile_picked_zbloom_none_po_kernel(
         w1_raw = [load_half(w1, 0, "w1_raw0")]
         offsets = sb.tile([P, S // 16], U16, name="offsets")
         nc.sync.dma_start(offsets[:], offs)
-        for j in range(4):
-            nc.sync.dma_start(
-                out=scale_table[j:P:32, :].bitcast(I32),
-                in_=x_scales[0, j:16:4, :].bitcast(I32),
-            )
+        nc.sync.dma_start(out=scale_table[0:P:8, :].bitcast(I32), in_=x_scales[0].bitcast(I32))
         nc.sync.dma_start(out=gate_rows[0:D, :], in_=gate[:, 0, :])
         word_table = sb.tile([P, T], U32, name="word_table", align_bytes=64)
         nc.sync.dma_start(
@@ -61,7 +57,6 @@ def tile_picked_zbloom_none_po_kernel(
             in_=x_words[0].rearrange("p n t -> p (n t)").bitcast(I32),
         )
         w1_raw.append(load_half(w1, 1, "w1_raw1"))
-        w2_raw = [load_half(w2, part, "w2_raw%d" % part) for part in range(2)]
 
         ident = sb.tile([P, P], F32, name="ident", align_bytes=64)
         make_identity(nc, ident[:])
@@ -85,8 +80,14 @@ def tile_picked_zbloom_none_po_kernel(
         gate_col = sb.tile([P, HALVES, D], F32, name="gate_col", align_bytes=64)
         nc.scalar.activation(gate_col[:], gate_ps[:, :, 0:D], COPY)
 
+        picked_sc = sb.tile([P, S], U8, name="picked_sc", align_bytes=64)
+        nc.vector.tensor_copy(picked_sc[:], scale_table[:].indirect(offsets[:]))
         x_sc = sb.tile([P, S], U8, name="x_sc", align_bytes=64)
-        nc.vector.tensor_copy(x_sc[:], scale_table[:].indirect(offsets[:]))
+        nc.gpsimd.memset(x_sc[:].bitcast(I32), 0)
+        for j in range(4):
+            nc.sync.dma_start(out=x_sc[j:P:32, :].bitcast(I32), in_=picked_sc[8 * j : P : 32, :].bitcast(I32))
+        w2_raw = sb.tile([P, PACK, N], F32, name="w2_raw", tag="w2_raw", align_bytes=64)
+        nc.sync.dma_start(out=w2_raw[:], in_=w2.rearrange("(p j) c -> p j c", j=PACK))
         x_w = []
         for a in range(2):
             picked = sb.tile([P, S // 2], U32, name="x_w%d" % a, align_bytes=64)
@@ -162,7 +163,7 @@ def tile_picked_zbloom_none_po_kernel(
             for part in range(2):
                 nc.scalar.copy(
                     out=rounded[:, :, part * 64 : (part + 1) * 64, :].rearrange("p e m j -> p m e j"),
-                    in_=w2_raw[part][:].rearrange("p j (m u e) -> p u m e j", u=2, e=2)[:, pair],
+                    in_=w2_raw[:, :, part * HALF : (part + 1) * HALF].rearrange("p j (m u e) -> p u m e j", u=2, e=2)[:, pair],
                 )
             tag = "three1" if pair == 1 else "acc110"
             codes = sb.tile([P, HALF], U32, name="w2_codes%d" % pair, tag=tag, align_bytes=64)

@@ -36,7 +36,8 @@ def tile_picked_zbloom_none_po_kernel(
             return ps.tile(shape, F32, name=name, tag="bank%d" % b)
 
         scale_table = sb.tile([P, T], U8, name="scale_table", tag="w2_raw", align_bytes=64)
-        nc.gpsimd.memset(scale_table[:].bitcast(I32), 0)
+        nc.gpsimd.memset(scale_table[:, : T // 2].bitcast(I32), 0)
+        nc.vector.memset(scale_table[:, T // 2 :].bitcast(I32), 0)
         gate_rows = sb.tile([P, V], F32, name="gate_rows", align_bytes=64)
         nc.gpsimd.memset(gate_rows[:], 0.0)
 
@@ -50,12 +51,12 @@ def tile_picked_zbloom_none_po_kernel(
         offsets = sb.tile([P, S // 16], U16, name="offsets")
         nc.sync.dma_start(offsets[:], offs)
         nc.sync.dma_start(out=scale_table[0:P:8, :].bitcast(I32), in_=x_scales[0].bitcast(I32))
-        nc.sync.dma_start(out=gate_rows[0:D, :], in_=gate[:, 0, :])
         word_table = sb.tile([P, T], U32, name="word_table", align_bytes=64)
         nc.sync.dma_start(
             out=word_table[:].bitcast(I32),
             in_=x_words[0].rearrange("p n t -> p (n t)").bitcast(I32),
         )
+        nc.sync.dma_start(out=gate_rows[0:D, :], in_=gate[:, 0, :])
         w1_raw.append(load_half(w1, 1, "w1_raw1"))
 
         ident = sb.tile([P, P], F32, name="ident", align_bytes=64)
@@ -64,8 +65,8 @@ def tile_picked_zbloom_none_po_kernel(
         def quantise_w1(part):
             rounded = sb.tile([P, HALF * PACK], BF16, name="w1_bf%d" % part, align_bytes=64)
             nc.scalar.copy(
-                out=rounded[:].rearrange("p (u q e j) -> p q u e j", u=2, e=2, j=PACK),
-                in_=w1_raw[part][:].rearrange("p j (q u e) -> p q u e j", u=2, e=2),
+                out=rounded[:].rearrange("p (u q e j) -> p q j u e", u=2, e=2, j=PACK),
+                in_=w1_raw[part][:].rearrange("p j (q u e) -> p q j u e", u=2, e=2),
             )
             codes = sb.tile([P, HALF], U32, name="w1_codes%d" % part, align_bytes=64)
             scales = sb.tile([P, HALF], U8, name="w1_scales%d" % part, align_bytes=64)
@@ -162,8 +163,8 @@ def tile_picked_zbloom_none_po_kernel(
             rounded = sb.tile([P, 2, P, PACK], BF16, name="w2_bf%d" % pair, align_bytes=64)
             for part in range(2):
                 nc.scalar.copy(
-                    out=rounded[:, :, part * 64 : (part + 1) * 64, :].rearrange("p e m j -> p m e j"),
-                    in_=w2_raw[:, :, part * HALF : (part + 1) * HALF].rearrange("p j (m u e) -> p u m e j", u=2, e=2)[:, pair],
+                    out=rounded[:, :, part * 64 : (part + 1) * 64, :].rearrange("p e m j -> p m j e"),
+                    in_=w2_raw[:, :, part * HALF : (part + 1) * HALF].rearrange("p j (m u e) -> p u m j e", u=2, e=2)[:, pair],
                 )
             tag = "three1" if pair == 1 else "acc110"
             codes = sb.tile([P, HALF], U32, name="w2_codes%d" % pair, tag=tag, align_bytes=64)

@@ -8,6 +8,7 @@ P = 128
 PACK = 4
 HALVES = V // P
 HALF = 256
+Q = HALF // PACK
 
 FLOPS = 2 * K * H * S + 2 * H * N * V
 BYTES = P * T * PACK + 16 * T + 4 * K * H + 4 * H * N + 4 * D * V + 2 * P * S // 16 + 4 * N * V + N * V + 16 * V
@@ -35,14 +36,17 @@ def tile_picked_zbloom_none_po_kernel(
         def bank(b, shape, name):
             return ps.tile(shape, F32, name=name, tag="bank%d" % b)
 
-        scale_table = sb.tile([P, T], U8, name="scale_table", tag="w2_raw", align_bytes=64)
+        def tile(shape, dtype, name, tag=None):
+            return sb.tile(shape, dtype, name=name, tag=tag or name, align_bytes=64)
+
+        gate_rows = tile([P, V], F32, "gate_rows")
+        nc.gpsimd.memset(gate_rows[:], 0.0)
+        scale_table = tile([P, T], U8, "scale_table", "w2_raw0")
         nc.gpsimd.memset(scale_table[:, : T // 2].bitcast(I32), 0)
         nc.vector.memset(scale_table[:, T // 2 :].bitcast(I32), 0)
-        gate_rows = sb.tile([P, V], F32, name="gate_rows", align_bytes=64)
-        nc.gpsimd.memset(gate_rows[:], 0.0)
 
         def load_half(weight, part, name):
-            raw = sb.tile([P, PACK, HALF], F32, name=name, tag=name, align_bytes=64)
+            raw = tile([P, PACK, HALF], F32, name)
             view = weight.rearrange("(p j) c -> p j c", j=PACK)
             nc.sync.dma_start(out=raw[:], in_=view[:, :, part * HALF : (part + 1) * HALF])
             return raw
@@ -51,177 +55,255 @@ def tile_picked_zbloom_none_po_kernel(
         offsets = sb.tile([P, S // 16], U16, name="offsets")
         nc.sync.dma_start(offsets[:], offs)
         nc.sync.dma_start(out=scale_table[0:P:8, :].bitcast(I32), in_=x_scales[0].bitcast(I32))
-        word_table = sb.tile([P, T], U32, name="word_table", align_bytes=64)
-        nc.sync.dma_start(
-            out=word_table[:].bitcast(I32),
-            in_=x_words[0].rearrange("p n t -> p (n t)").bitcast(I32),
-        )
+        word_table = tile([P, T], U32, "word_table")
+        words_in = x_words[0].rearrange("p n t -> p (n t)").bitcast(I32)
+        first = 3 * T // 4
+        nc.sync.dma_start(out=word_table[:, :first].bitcast(I32), in_=words_in[:, :first])
         nc.sync.dma_start(out=gate_rows[0:D, :], in_=gate[:, 0, :])
+        nc.sync.dma_start(out=word_table[:, first:].bitcast(I32), in_=words_in[:, first:])
         w1_raw.append(load_half(w1, 1, "w1_raw1"))
 
-        ident = sb.tile([P, P], F32, name="ident", align_bytes=64)
+        ident = tile([P, P], F32, "ident")
         make_identity(nc, ident[:])
 
-        def quantise_w1(part):
-            rounded = sb.tile([P, HALF * PACK], BF16, name="w1_bf%d" % part, align_bytes=64)
+        def round_w1(part):
+            rounded = tile([P, HALF * PACK], BF16, "w1_bf%d" % part)
             nc.scalar.copy(
-                out=rounded[:].rearrange("p (u q e j) -> p q j u e", u=2, e=2, j=PACK),
-                in_=w1_raw[part][:].rearrange("p j (q u e) -> p q j u e", u=2, e=2),
+                out=rounded[:].rearrange("p (q t j) -> p q j t", t=PACK, j=PACK),
+                in_=w1_raw[part][:].rearrange("p j (q t) -> p q j t", t=PACK),
             )
-            codes = sb.tile([P, HALF], U32, name="w1_codes%d" % part, align_bytes=64)
-            scales = sb.tile([P, HALF], U8, name="w1_scales%d" % part, align_bytes=64)
+            return rounded
+
+        def quantise_w1(part, rounded):
+            codes = tile([P, HALF], U32, "w1_codes%d" % part)
+            scales = tile([P, HALF], U8, "w1_scales%d" % part)
             nc.vector.quantize_mx(out=codes[:].bitcast(FP8X4), scales=scales[:], in_=rounded[:])
             return codes, scales
 
-        w1_mx = [quantise_w1(0)]
+        w1_first = round_w1(0)
 
         gate_ps = bank(7, [P, HALVES, P], "gate_ps")
         for h in range(HALVES):
             nc.tensor.transpose(gate_ps[:, h, :], gate_rows[:, h * P : (h + 1) * P], ident[:])
-        gate_col = sb.tile([P, HALVES, D], F32, name="gate_col", align_bytes=64)
+        gate_col = tile([P, HALVES, D], F32, "gate_col")
         nc.scalar.activation(gate_col[:], gate_ps[:, :, 0:D], COPY)
 
-        picked_sc = sb.tile([P, S], U8, name="picked_sc", align_bytes=64)
+        picked_sc = tile([P, S], U8, "picked_sc")
         nc.vector.tensor_copy(picked_sc[:], scale_table[:].indirect(offsets[:]))
-        x_sc = sb.tile([P, S], U8, name="x_sc", align_bytes=64)
+        w1_mx = [quantise_w1(0, w1_first)]
+        x_sc = tile([P, S], U8, "x_sc")
         nc.gpsimd.memset(x_sc[:].bitcast(I32), 0)
         for j in range(4):
             nc.sync.dma_start(out=x_sc[j:P:32, :].bitcast(I32), in_=picked_sc[8 * j : P : 32, :].bitcast(I32))
-        w2_raw = sb.tile([P, PACK, N], F32, name="w2_raw", tag="w2_raw", align_bytes=64)
-        nc.sync.dma_start(out=w2_raw[:], in_=w2.rearrange("(p j) c -> p j c", j=PACK))
+        w2_both = tile([P, 2, PACK, HALF], F32, "w2_both", "w2_raw0")
+        w2_raw = [w2_both[:, part] for part in range(2)]
+        for part in range(2):
+            nc.sync.dma_start(
+                out=w2_raw[part], in_=w2.rearrange("(p j) c -> p j c", j=PACK)[:, :, part * HALF : (part + 1) * HALF]
+            )
         x_w = []
         for a in range(2):
-            picked = sb.tile([P, S // 2], U32, name="x_w%d" % a, align_bytes=64)
+            picked = tile([P, S // 2], U32, "x_w%d" % a)
             nc.vector.tensor_copy(picked[:], word_table[:].indirect(offsets[:, a * 32 : (a + 1) * 32]))
             x_w.append(picked)
-        w1_mx.append(quantise_w1(1))
 
-        def first_product(out, d, h, part, lo, hi):
-            codes, scales = w1_mx[part]
-            first = d * V + h * P
-            local = first % (S // 2)
+        warm = bank(7, [P, HALF], "warm")
+        for turn in range(5):
             nc.tensor.matmul_mx(
-                out=out,
-                lhsT=x_w[d // 2][:, local : local + P].bitcast(FP8X4),
-                lhsT_scale=x_sc[:, first : first + P],
-                rhs=codes[:, lo:hi].bitcast(FP8X4),
-                rhs_scale=scales[:, lo:hi],
+                out=warm[:],
+                lhsT=w1_mx[0][0][:, :P].bitcast(FP8X4),
+                lhsT_scale=w1_mx[0][1][:, :P],
+                rhs=w1_mx[0][0][:].bitcast(FP8X4),
+                rhs_scale=w1_mx[0][1][:],
                 start=True,
                 stop=True,
             )
 
+        def deal(copy, rounded, raw, lo, hi, at):
+            copy(
+                out=rounded[:, :, at + lo : at + hi, :].rearrange("p t q j -> p q j t"),
+                in_=raw.rearrange("p j (q t) -> p q j t", t=PACK)[:, lo:hi],
+            )
+
+        w1_mx.append(quantise_w1(1, round_w1(1)))
+
+        pairs = (
+            ((0, 1, 0), (0, 0, 0)),
+            ((1, 0, 0), (3, 0, 0)),
+            ((0, 1, 1), (0, 0, 1)),
+            ((1, 0, 1), (3, 0, 1)),
+            ((1, 1, 0), (2, 0, 0)),
+            ((2, 1, 0), (3, 1, 0)),
+            ((1, 1, 1), (2, 0, 1)),
+            ((2, 1, 1), (3, 1, 1)),
+        )
         y = {}
-        for d, part in ((0, 0), (1, 0), (2, 0), (0, 1), (1, 1), (2, 1)):
-            y[d, part] = bank(2 * d + part, [P, HALVES, HALF], "y%d%d" % (d, part))
-            for h in range(HALVES):
-                first_product(y[d, part][:, h, :], d, h, part, 0, HALF)
-        y_last = []
-        for h in range(HALVES):
-            y_last.append(bank(2 * h, [P, 2, 2, P], "y_last%d" % h))
-            for part in range(2):
-                for u in range(2):
-                    first_product(y_last[h][:, u, part, :], D - 1, h, part, u * P, (u + 1) * P)
+        for b, pair in enumerate(pairs):
+            both = bank(b, [P, 2, HALF], "y%d" % b)
+            for e, piece in enumerate(pair):
+                y[piece] = both[:, e, :]
+        passes = (
+            (0, 1, 0), (0, 0, 0), (1, 0, 0), (1, 1, 0), (2, 0, 0), (3, 0, 0), (2, 1, 0), (3, 1, 0),
+            (0, 1, 1), (0, 0, 1), (1, 1, 1), (2, 0, 1), (1, 0, 1), (3, 0, 1), (2, 1, 1), (3, 1, 1),
+        )
+        for d, h, part in passes:
+            codes, scales = w1_mx[part]
+            at = d * V + h * P
+            local = at % (S // 2)
+            nc.tensor.matmul_mx(
+                out=y[d, h, part],
+                lhsT=x_w[d // 2][:, local : local + P].bitcast(FP8X4),
+                lhsT_scale=x_sc[:, at : at + P],
+                rhs=codes[:].bitcast(FP8X4),
+                rhs_scale=scales[:],
+                start=True,
+                stop=True,
+            )
 
-        three = [sb.tile([P, 2, 2, P], F32, name="three%d" % h, tag="three%d" % h, align_bytes=64) for h in range(HALVES)]
-        for part in range(2):
-            acc = {}
-            for d in range(D - 1):
-                for h in range(HALVES):
-                    factor = gate_col[:, h, d : d + 1]
-                    name = "acc%d%d%d" % (part, h, d)
-                    if d == D - 2:
-                        nc.vector.scalar_tensor_tensor(
-                            three[h][:, :, part, :],
-                            y[d, part][:, h, :].rearrange("p (u c) -> p u c", u=2),
-                            factor,
-                            acc[h][:].rearrange("p (u c) -> p u c", u=2),
-                            MULT,
-                            ADD,
-                        )
-                        continue
-                    tag = {"acc000": "w1_raw1", "acc101": "acc011"}.get(name, name)
-                    nxt = sb.tile([P, HALF], F32, name=name, tag=tag, align_bytes=64)
-                    if d == 0:
-                        nc.scalar.activation(nxt[:], y[d, part][:, h, :], COPY, scale=factor)
-                    else:
-                        nc.vector.scalar_tensor_tensor(nxt[:], y[d, part][:, h, :], factor, acc[h][:], MULT, ADD)
-                    acc[h] = nxt
-        z_rows = []
-        for h in range(HALVES):
-            z_rows.append(sb.tile([P, H], BF16, name="z_rows%d" % h, align_bytes=64))
+        terms = [tile([P, PACK, P], F32, "term%d" % e) for e in range(3)]
+        z_rows = tile([P, 2, P, 2], BF16, "z_rows")
+        acc = {}
+
+        def dealt(d, part):
+            return y[d, 0, part].rearrange("p (q t) -> p t q", t=PACK)
+
+        def scale_first(h, part):
+            if h == 0:
+                acc[0, part] = tile([P, PACK, Q], F32, "acc0%d" % part)
+                nc.scalar.activation(acc[0, part][:], dealt(0, part), COPY, scale=gate_col[:, 0, 0:1])
+            else:
+                acc[1, part] = tile([P, HALF], F32, "acc1%d" % part)
+                nc.scalar.activation(acc[1, part][:], y[0, 1, part], COPY, scale=gate_col[:, 1, 0:1])
+
+        def own_term(e, d, part):
+            nc.scalar.activation(
+                terms[e][:, :, part * Q : (part + 1) * Q], dealt(d, part), COPY, scale=gate_col[:, 0, d : d + 1]
+            )
+
+        def add_term(part):
             nc.vector.scalar_tensor_tensor(
-                z_rows[h][:],
-                y_last[h][:].rearrange("p u a c -> p (u a c)"),
-                gate_col[:, h, D - 1 : D],
-                three[h][:].rearrange("p u a c -> p (u a c)"),
-                MULT,
-                ADD,
+                terms[2][:, :, part * Q : (part + 1) * Q], dealt(2, part), gate_col[:, 0, 2:3], acc[0, part][:], MULT, ADD
             )
 
-        w2_mx = []
-        for pair in range(2):
-            rounded = sb.tile([P, 2, P, PACK], BF16, name="w2_bf%d" % pair, align_bytes=64)
-            for part in range(2):
-                nc.scalar.copy(
-                    out=rounded[:, :, part * 64 : (part + 1) * 64, :].rearrange("p e m j -> p m j e"),
-                    in_=w2_raw[:, :, part * HALF : (part + 1) * HALF].rearrange("p j (m u e) -> p u m j e", u=2, e=2)[:, pair],
+        def chain(d, part):
+            nxt = tile([P, HALF], F32, "chain%d%d" % (d, part))
+            nc.vector.scalar_tensor_tensor(
+                nxt[:], y[d, 1, part], gate_col[:, 1, d : d + 1], acc[1, part][:], MULT, ADD
+            )
+            acc[1, part] = nxt
+
+        def chain_end(part):
+            for u in range(2):
+                nc.vector.scalar_tensor_tensor(
+                    z_rows[:, u, part * Q : (part + 1) * Q, :],
+                    y[3, 1, part].rearrange("p (q u e) -> p u q e", u=2, e=2)[:, u],
+                    gate_col[:, 1, 3:4],
+                    acc[1, part][:].rearrange("p (q u e) -> p u q e", u=2, e=2)[:, u],
+                    MULT,
+                    ADD,
                 )
-            tag = "three1" if pair == 1 else "acc110"
-            codes = sb.tile([P, HALF], U32, name="w2_codes%d" % pair, tag=tag, align_bytes=64)
-            scales = sb.tile([P, HALF], U8, name="w2_scales%d" % pair, align_bytes=64)
-            nc.vector.quantize_mx(
-                out=codes[:].bitcast(FP8X4), scales=scales[:], in_=rounded[:].rearrange("p e m j -> p (e m j)")
-            )
-            w2_mx.append((codes, scales))
 
-        z_codes = sb.tile([P, V], U32, name="z_codes", align_bytes=64)
-        z_scales = sb.tile([P, V], U8, name="z_scales", align_bytes=64)
+        scale_first(1, 0)
+        scale_first(0, 0)
+        own_term(0, 1, 0)
+        own_term(1, 3, 0)
+        scale_first(1, 1)
+        scale_first(0, 1)
+        own_term(0, 1, 1)
+        own_term(1, 3, 1)
+        chain(1, 0)
+        add_term(0)
+        chain(2, 0)
+        chain_end(0)
+        chain(1, 1)
+        add_term(1)
+        chain(2, 1)
+        chain_end(1)
+
+        z_sum = bank(0, [P, PACK, P], "z_sum")
+        for n, e in enumerate((0, 1, 2)):
+            for t in range(PACK):
+                nc.tensor.matmul(
+                    z_sum[:, t, :],
+                    lhsT=terms[e][:, t, :],
+                    rhs=ident[:],
+                    is_transpose=True,
+                    start=(n == 0 and t == 0),
+                    stop=(n == 2 and t == PACK - 1),
+                )
+        z_pairs = bank(4, [P, 2, P], "z_pairs")
+        for u in range(2):
+            nc.tensor.transpose(
+                z_pairs[:, u, :], z_rows[:, u].rearrange("p q e -> p (q e)").bitcast(F32), ident[:]
+            )
+
+        w2_codes = tile([P, N], U32, "w2_codes")
+        w2_scales = tile([P, N], U8, "w2_scales")
+        for part in range(2):
+            rounded = tile([P, PACK, Q, PACK], BF16, "w2_bf%d" % part, ("w1_bf1", "chain21")[part])
+            if part == 0:
+                nc.gpsimd.tensor_copy(out=rounded[:], in_=w2_raw[0].rearrange("p j (q t) -> p t q j", t=PACK))
+            else:
+                deal(nc.vector.tensor_copy, rounded, w2_raw[1], 0, Q, 0)
+            for t in range(PACK):
+                cols = slice(t * P + part * Q, t * P + (part + 1) * Q)
+                nc.vector.quantize_mx(
+                    out=w2_codes[:, cols].bitcast(FP8X4),
+                    scales=w2_scales[:, cols],
+                    in_=rounded[:, t].rearrange("p q j -> p (q j)"),
+                )
+
+        z_codes = tile([P, V], U32, "z_codes")
+        z_scales = tile([P, V], U8, "z_scales")
         for h in range(HALVES):
             cols = slice(h * P, (h + 1) * P)
-            z_ps = bank(6 + h, [P, 2, P], "z_ps%d" % h)
-            pairs = z_rows[h][:].bitcast(F32)
-            for u in range(2):
-                nc.tensor.transpose(z_ps[:, u, :], pairs[:, u * P : (u + 1) * P], ident[:])
-            z_bf = sb.tile([P, P * PACK], BF16, name="z_bf%d" % h, align_bytes=64)
-            nc.scalar.copy(
-                out=z_bf[:].bitcast(F32).rearrange("p (v u) -> p v u", u=2),
-                in_=z_ps[:].rearrange("p u v -> p v u"),
-            )
+            z_bf = tile([P, P * PACK], BF16, "z_bf%d" % h)
+            if h == 0:
+                nc.scalar.copy(
+                    out=z_bf[:].rearrange("p (v t) -> p v t", t=PACK),
+                    in_=z_sum[:].rearrange("p t v -> p v t"),
+                )
+            else:
+                nc.scalar.copy(
+                    out=z_bf[:].bitcast(F32).rearrange("p (v u) -> p v u", u=2),
+                    in_=z_pairs[:].rearrange("p u v -> p v u"),
+                )
             nc.vector.quantize_mx(out=z_codes[:, cols].bitcast(FP8X4), scales=z_scales[:, cols], in_=z_bf[:])
 
-        out_codes = sb.tile([P, V], U32, name="out_codes", align_bytes=64)
-        out_scales = sb.tile([P, V], U8, name="out_scales", align_bytes=64)
+        out_codes = tile([P, V], U32, "out_codes")
+        out_scales = tile([P, V], U8, "out_scales")
         out_view = out_0.rearrange("(p t) v -> p t v", t=PACK)
-        o_ps = []
+        o_f32 = []
         for h in range(HALVES):
             cols = slice(h * P, (h + 1) * P)
-            o_ps.append(bank(2 * h + 1, [P, PACK, P], "o_ps%d" % h))
-            for t in range(PACK):
-                nc.tensor.matmul_mx(
-                    out=o_ps[h][:, t, :],
-                    lhsT=w2_mx[t // 2][0][:, t % 2 * P : (t % 2 + 1) * P].bitcast(FP8X4),
-                    lhsT_scale=w2_mx[t // 2][1][:, t % 2 * P : (t % 2 + 1) * P],
-                    rhs=z_codes[:, cols].bitcast(FP8X4),
-                    rhs_scale=z_scales[:, cols],
-                    start=True,
-                    stop=True,
-                )
-        o_bf = []
+            o_f32.append(tile([P, PACK, P], F32, "o_f32%d" % h))
+            for pair in range(2):
+                o_ps = bank(1 + h + 4 * pair, [P, 2, P], "o_ps%d%d" % (h, pair))
+                for e in range(2):
+                    t = 2 * pair + e
+                    nc.tensor.matmul_mx(
+                        out=o_ps[:, e, :],
+                        lhsT=w2_codes[:, t * P : (t + 1) * P].bitcast(FP8X4),
+                        lhsT_scale=w2_scales[:, t * P : (t + 1) * P],
+                        rhs=z_codes[:, cols].bitcast(FP8X4),
+                        rhs_scale=z_scales[:, cols],
+                        start=True,
+                        stop=True,
+                    )
+                copy = (nc.scalar.copy, nc.vector.tensor_copy)[pair]
+                copy(out=o_f32[h][:, 2 * pair : 2 * pair + 2, :], in_=o_ps[:])
+            nc.sync.dma_start(out=out_view[:, :, cols], in_=o_f32[h][:])
+        o_bf = tile([P, HALVES, P * PACK], BF16, "o_bf")
         for h in range(HALVES):
-            o_bf.append(sb.tile([P, P * PACK], BF16, name="o_bf%d" % h, align_bytes=64))
-            round_out = nc.scalar.copy if h == 0 else nc.vector.tensor_copy
-            round_out(
-                out=o_bf[h][:].rearrange("p (v t) -> p v t", t=PACK),
-                in_=o_ps[h][:].rearrange("p t v -> p v t"),
+            copy = (nc.scalar.copy, nc.vector.tensor_copy)[h]
+            copy(
+                out=o_bf[:, h, :].rearrange("p (c i t) -> p c t i", t=PACK, i=4),
+                in_=o_f32[h][:].rearrange("p t (c i) -> p c t i", i=4),
             )
-        for h in range(HALVES):
-            cols = slice(h * P, (h + 1) * P)
-            nc.vector.quantize_mx(out=out_codes[:, cols].bitcast(FP8X4), scales=out_scales[:, cols], in_=o_bf[h][:])
-            o_f32 = sb.tile([P, PACK, P], F32, name="o_f32%d" % h, align_bytes=64)
-            nc.scalar.copy(out=o_f32[:], in_=o_ps[h][:])
-            queue = nc.sync if h == 0 else nc.scalar
-            queue.dma_start(out=out_view[:, :, cols], in_=o_f32[:])
-        nc.sync.dma_start(
+        nc.vector.quantize_mx(
+            out=out_codes[:].bitcast(FP8X4), scales=out_scales[:], in_=o_bf[:].rearrange("p h c -> p (h c)")
+        )
+        nc.scalar.dma_start(
             out=out_1[0].rearrange("p n t -> p (n t)").bitcast(I32),
             in_=out_codes[:].bitcast(I32),
         )

@@ -129,24 +129,23 @@ def tile_picked_zbloom_none_po_kernel(
 
         pairs = (
             ((0, 1, 0), (0, 0, 0)),
-            ((1, 0, 0), (3, 0, 0)),
+            ((1, 0, 0), (1, 0, 1)),
             ((0, 1, 1), (0, 0, 1)),
-            ((1, 0, 1), (3, 0, 1)),
-            ((1, 1, 0), (2, 0, 0)),
-            ((2, 1, 0), (3, 1, 0)),
-            ((1, 1, 1), (2, 0, 1)),
-            ((2, 1, 1), (3, 1, 1)),
+            ((2, 0, 0), (2, 0, 1)),
+            ((3, 0, 0), (3, 0, 1)),
+            ((1, 1, 0), (2, 1, 0)),
+            ((3, 1, 0), (3, 1, 1)),
+            ((1, 1, 1), (2, 1, 1)),
         )
         y = {}
+        banks = []
         for b, pair in enumerate(pairs):
             both = bank(b, [P, 2, HALF], "y%d" % b)
+            banks.append(both)
             for e, piece in enumerate(pair):
                 y[piece] = both[:, e, :]
-        passes = (
-            (0, 1, 0), (0, 0, 0), (1, 0, 0), (1, 1, 0), (2, 0, 0), (3, 0, 0), (2, 1, 0), (3, 1, 0),
-            (0, 1, 1), (0, 0, 1), (1, 1, 1), (2, 0, 1), (1, 0, 1), (3, 0, 1), (2, 1, 1), (3, 1, 1),
-        )
-        for d, h, part in passes:
+
+        def first_product(d, h, part):
             codes, scales = w1_mx[part]
             at = d * V + h * P
             local = at % (S // 2)
@@ -160,37 +159,26 @@ def tile_picked_zbloom_none_po_kernel(
                 stop=True,
             )
 
-        terms = [tile([P, PACK, P], F32, "term%d" % e) for e in range(3)]
+        terms = [tile([P, PACK, P], F32, "term%d" % d) for d in range(D)]
         z_rows = tile([P, 2, P, 2], BF16, "z_rows")
         acc = {}
 
-        def dealt(d, part):
-            return y[d, 0, part].rearrange("p (q t) -> p t q", t=PACK)
+        def scale_first(part):
+            acc[part] = tile([P, HALF], F32, "acc%d" % part)
+            nc.scalar.activation(acc[part][:], y[0, 1, part], COPY, scale=gate_col[:, 1, 0:1])
 
-        def scale_first(h, part):
-            if h == 0:
-                acc[0, part] = tile([P, PACK, Q], F32, "acc0%d" % part)
-                nc.scalar.activation(acc[0, part][:], dealt(0, part), COPY, scale=gate_col[:, 0, 0:1])
-            else:
-                acc[1, part] = tile([P, HALF], F32, "acc1%d" % part)
-                nc.scalar.activation(acc[1, part][:], y[0, 1, part], COPY, scale=gate_col[:, 1, 0:1])
-
-        def own_term(e, d, part):
+        def own_term(d, part):
             nc.scalar.activation(
-                terms[e][:, :, part * Q : (part + 1) * Q], dealt(d, part), COPY, scale=gate_col[:, 0, d : d + 1]
-            )
-
-        def add_term(part):
-            nc.vector.scalar_tensor_tensor(
-                terms[2][:, :, part * Q : (part + 1) * Q], dealt(2, part), gate_col[:, 0, 2:3], acc[0, part][:], MULT, ADD
+                terms[d][:, :, part * Q : (part + 1) * Q],
+                y[d, 0, part].rearrange("p (q t) -> p t q", t=PACK),
+                COPY,
+                scale=gate_col[:, 0, d : d + 1],
             )
 
         def chain(d, part):
             nxt = tile([P, HALF], F32, "chain%d%d" % (d, part))
-            nc.vector.scalar_tensor_tensor(
-                nxt[:], y[d, 1, part], gate_col[:, 1, d : d + 1], acc[1, part][:], MULT, ADD
-            )
-            acc[1, part] = nxt
+            nc.vector.scalar_tensor_tensor(nxt[:], y[d, 1, part], gate_col[:, 1, d : d + 1], acc[part][:], MULT, ADD)
+            acc[part] = nxt
 
         def chain_end(part):
             for u in range(2):
@@ -198,53 +186,57 @@ def tile_picked_zbloom_none_po_kernel(
                     z_rows[:, u, part * Q : (part + 1) * Q, :],
                     y[3, 1, part].rearrange("p (q u e) -> p u q e", u=2, e=2)[:, u],
                     gate_col[:, 1, 3:4],
-                    acc[1, part][:].rearrange("p (q u e) -> p u q e", u=2, e=2)[:, u],
+                    acc[part][:].rearrange("p (q u e) -> p u q e", u=2, e=2)[:, u],
                     MULT,
                     ADD,
                 )
 
-        scale_first(1, 0)
-        scale_first(0, 0)
-        own_term(0, 1, 0)
-        own_term(1, 3, 0)
-        scale_first(1, 1)
-        scale_first(0, 1)
-        own_term(0, 1, 1)
-        own_term(1, 3, 1)
+        for d, h in ((0, 1), (0, 0), (1, 0), (1, 1), (2, 1), (3, 1), (2, 0), (3, 0)):
+            first_product(d, h, 0)
+        scale_first(0)
+        own_term(0, 0)
+        own_term(1, 0)
+        for d, h in ((0, 1), (0, 0), (1, 1), (2, 1), (3, 1), (1, 0), (2, 0), (3, 0)):
+            first_product(d, h, 1)
+        scale_first(1)
+        own_term(0, 1)
+        own_term(1, 1)
+        for d in (2, 3):
+            nc.scalar.activation(
+                terms[d][:],
+                banks[d + 1][:].rearrange("p a (q t) -> p t (a q)", t=PACK),
+                COPY,
+                scale=gate_col[:, 0, d : d + 1],
+            )
         chain(1, 0)
-        add_term(0)
         chain(2, 0)
-        chain_end(0)
         chain(1, 1)
-        add_term(1)
+        chain_end(0)
         chain(2, 1)
         chain_end(1)
 
         z_sum = bank(0, [P, PACK, P], "z_sum")
-        for n, e in enumerate((0, 1, 2)):
+        for d in range(D):
             for t in range(PACK):
                 nc.tensor.matmul(
                     z_sum[:, t, :],
-                    lhsT=terms[e][:, t, :],
+                    lhsT=terms[d][:, t, :],
                     rhs=ident[:],
                     is_transpose=True,
-                    start=(n == 0 and t == 0),
-                    stop=(n == 2 and t == PACK - 1),
+                    start=(d == 0 and t == 0),
+                    stop=(d == D - 1 and t == PACK - 1),
                 )
-        z_pairs = bank(4, [P, 2, P], "z_pairs")
+        z_pairs = bank(5, [P, 2, P], "z_pairs")
         for u in range(2):
             nc.tensor.transpose(
                 z_pairs[:, u, :], z_rows[:, u].rearrange("p q e -> p (q e)").bitcast(F32), ident[:]
             )
 
-        w2_codes = tile([P, N], U32, "w2_codes")
+        w2_codes = tile([P, N], U32, "w2_codes", "chain11")
         w2_scales = tile([P, N], U8, "w2_scales")
         for part in range(2):
-            rounded = tile([P, PACK, Q, PACK], BF16, "w2_bf%d" % part, ("w1_bf1", "chain21")[part])
-            if part == 0:
-                nc.gpsimd.tensor_copy(out=rounded[:], in_=w2_raw[0].rearrange("p j (q t) -> p t q j", t=PACK))
-            else:
-                deal(nc.vector.tensor_copy, rounded, w2_raw[1], 0, Q, 0)
+            rounded = tile([P, PACK, Q, PACK], BF16, "w2_bf%d" % part, ("acc0", "chain21")[part])
+            deal(nc.vector.tensor_copy, rounded, w2_raw[part], 0, Q, 0)
             for t in range(PACK):
                 cols = slice(t * P + part * Q, t * P + (part + 1) * Q)
                 nc.vector.quantize_mx(
@@ -278,7 +270,7 @@ def tile_picked_zbloom_none_po_kernel(
             cols = slice(h * P, (h + 1) * P)
             o_f32.append(tile([P, PACK, P], F32, "o_f32%d" % h))
             for pair in range(2):
-                o_ps = bank(1 + h + 4 * pair, [P, 2, P], "o_ps%d%d" % (h, pair))
+                o_ps = bank(1 + h + 5 * pair, [P, 2, P], "o_ps%d%d" % (h, pair))
                 for e in range(2):
                     t = 2 * pair + e
                     nc.tensor.matmul_mx(
@@ -293,16 +285,17 @@ def tile_picked_zbloom_none_po_kernel(
                 copy = (nc.scalar.copy, nc.vector.tensor_copy)[pair]
                 copy(out=o_f32[h][:, 2 * pair : 2 * pair + 2, :], in_=o_ps[:])
             nc.sync.dma_start(out=out_view[:, :, cols], in_=o_f32[h][:])
-        o_bf = tile([P, HALVES, P * PACK], BF16, "o_bf")
+        o_bf = []
         for h in range(HALVES):
+            o_bf.append(tile([P, P * PACK], BF16, "o_bf%d" % h))
             copy = (nc.scalar.copy, nc.vector.tensor_copy)[h]
             copy(
-                out=o_bf[:, h, :].rearrange("p (c i t) -> p c t i", t=PACK, i=4),
+                out=o_bf[h][:].rearrange("p (c i t) -> p c t i", t=PACK, i=4),
                 in_=o_f32[h][:].rearrange("p t (c i) -> p c t i", i=4),
             )
-        nc.vector.quantize_mx(
-            out=out_codes[:].bitcast(FP8X4), scales=out_scales[:], in_=o_bf[:].rearrange("p h c -> p (h c)")
-        )
+        for h in range(HALVES):
+            cols = slice(h * P, (h + 1) * P)
+            nc.vector.quantize_mx(out=out_codes[:, cols].bitcast(FP8X4), scales=out_scales[:, cols], in_=o_bf[h][:])
         nc.scalar.dma_start(
             out=out_1[0].rearrange("p n t -> p (n t)").bitcast(I32),
             in_=out_codes[:].bitcast(I32),

@@ -87,6 +87,8 @@ def tile_picked_zbloom_none_po_kernel(
             nc.tensor.transpose(gate_ps[:, h, :], gate_rows[:, h * P : (h + 1) * P], ident[:])
         gate_col = tile([P, HALVES, D], F32, "gate_col")
         nc.scalar.activation(gate_col[:], gate_ps[:, :, 0:D], COPY)
+        gate_last = tile([P, 1], F32, "gate_last")
+        nc.scalar.activation(gate_last[:], gate_ps[:, 0, D - 1 : D], COPY)
 
         picked_sc = tile([P, S], U8, "picked_sc")
         nc.vector.tensor_copy(picked_sc[:], scale_table[:].indirect(offsets[:]))
@@ -127,23 +129,7 @@ def tile_picked_zbloom_none_po_kernel(
 
         w1_mx.append(quantise_w1(1, round_w1(1)))
 
-        pairs = (
-            ((0, 1, 0), (0, 0, 0)),
-            ((1, 0, 0), (1, 0, 1)),
-            ((0, 1, 1), (0, 0, 1)),
-            ((2, 0, 0), (2, 0, 1)),
-            ((3, 0, 0), (3, 0, 1)),
-            ((1, 1, 0), (2, 1, 0)),
-            ((3, 1, 0), (3, 1, 1)),
-            ((1, 1, 1), (2, 1, 1)),
-        )
         y = {}
-        banks = []
-        for b, pair in enumerate(pairs):
-            both = bank(b, [P, 2, HALF], "y%d" % b)
-            banks.append(both)
-            for e, piece in enumerate(pair):
-                y[piece] = both[:, e, :]
 
         def first_product(d, h, part):
             codes, scales = w1_mx[part]
@@ -165,14 +151,14 @@ def tile_picked_zbloom_none_po_kernel(
 
         def scale_first(part):
             acc[part] = tile([P, HALF], F32, "acc%d" % part)
-            nc.scalar.activation(acc[part][:], y[0, 1, part], COPY, scale=gate_col[:, 1, 0:1])
+            nc.vector.tensor_scalar(acc[part][:], y[0, 1, part], gate_col[:, 1, 0:1], None, MULT)
 
         def own_term(d, part):
             nc.scalar.activation(
                 terms[d][:, :, part * Q : (part + 1) * Q],
                 y[d, 0, part].rearrange("p (q t) -> p t q", t=PACK),
                 COPY,
-                scale=gate_col[:, 0, d : d + 1],
+                scale=gate_last[:] if d == D - 1 else gate_col[:, 0, d : d + 1],
             )
 
         def chain(d, part):
@@ -191,24 +177,19 @@ def tile_picked_zbloom_none_po_kernel(
                     ADD,
                 )
 
-        for d, h in ((0, 1), (0, 0), (1, 0), (1, 1), (2, 1), (3, 1), (2, 0), (3, 0)):
-            first_product(d, h, 0)
+        for part in range(2):
+            for pair in range(2):
+                for h in range(HALVES):
+                    both = bank(4 * part + 2 * pair + h, [P, 2, HALF], "y%d%d%d" % (part, pair, h))
+                    for e in range(2):
+                        y[2 * pair + e, h, part] = both[:, e, :]
+                        first_product(2 * pair + e, h, part)
+        for part in range(2):
+            for d in range(D):
+                own_term(d, part)
         scale_first(0)
-        own_term(0, 0)
-        own_term(1, 0)
-        for d, h in ((0, 1), (0, 0), (1, 1), (2, 1), (3, 1), (1, 0), (2, 0), (3, 0)):
-            first_product(d, h, 1)
-        scale_first(1)
-        own_term(0, 1)
-        own_term(1, 1)
-        for d in (2, 3):
-            nc.scalar.activation(
-                terms[d][:],
-                banks[d + 1][:].rearrange("p a (q t) -> p t (a q)", t=PACK),
-                COPY,
-                scale=gate_col[:, 0, d : d + 1],
-            )
         chain(1, 0)
+        scale_first(1)
         chain(2, 0)
         chain(1, 1)
         chain_end(0)
@@ -226,7 +207,7 @@ def tile_picked_zbloom_none_po_kernel(
                     start=(d == 0 and t == 0),
                     stop=(d == D - 1 and t == PACK - 1),
                 )
-        z_pairs = bank(5, [P, 2, P], "z_pairs")
+        z_pairs = bank(1, [P, 2, P], "z_pairs")
         for u in range(2):
             nc.tensor.transpose(
                 z_pairs[:, u, :], z_rows[:, u].rearrange("p q e -> p (q e)").bitcast(F32), ident[:]
@@ -235,8 +216,8 @@ def tile_picked_zbloom_none_po_kernel(
         w2_codes = tile([P, N], U32, "w2_codes", "chain11")
         w2_scales = tile([P, N], U8, "w2_scales")
         for part in range(2):
-            rounded = tile([P, PACK, Q, PACK], BF16, "w2_bf%d" % part, ("acc0", "chain21")[part])
-            deal(nc.vector.tensor_copy, rounded, w2_raw[part], 0, Q, 0)
+            rounded = tile([P, PACK, Q, PACK], BF16, "w2_bf%d" % part, ("w1_bf1", "gate_last")[part])
+            deal((nc.vector.tensor_copy, nc.scalar.copy)[part], rounded, w2_raw[part], 0, Q, 0)
             for t in range(PACK):
                 cols = slice(t * P + part * Q, t * P + (part + 1) * Q)
                 nc.vector.quantize_mx(
@@ -270,7 +251,7 @@ def tile_picked_zbloom_none_po_kernel(
             cols = slice(h * P, (h + 1) * P)
             o_f32.append(tile([P, PACK, P], F32, "o_f32%d" % h))
             for pair in range(2):
-                o_ps = bank(1 + h + 5 * pair, [P, 2, P], "o_ps%d%d" % (h, pair))
+                o_ps = bank(2 + 2 * h + pair, [P, 2, P], "o_ps%d%d" % (h, pair))
                 for e in range(2):
                     t = 2 * pair + e
                     nc.tensor.matmul_mx(
@@ -282,26 +263,21 @@ def tile_picked_zbloom_none_po_kernel(
                         start=True,
                         stop=True,
                     )
-                copy = (nc.scalar.copy, nc.vector.tensor_copy)[pair]
+                copy = nc.vector.tensor_copy if (h, pair) == (0, 1) else nc.scalar.copy
                 copy(out=o_f32[h][:, 2 * pair : 2 * pair + 2, :], in_=o_ps[:])
             nc.sync.dma_start(out=out_view[:, :, cols], in_=o_f32[h][:])
-        o_bf = []
-        for h in range(HALVES):
-            o_bf.append(tile([P, P * PACK], BF16, "o_bf%d" % h))
-            copy = (nc.scalar.copy, nc.vector.tensor_copy)[h]
-            copy(
-                out=o_bf[h][:].rearrange("p (c i t) -> p c t i", t=PACK, i=4),
+            o_bf = tile([P, P * PACK], BF16, "o_bf%d" % h)
+            nc.vector.tensor_copy(
+                out=o_bf[:].rearrange("p (c i t) -> p c t i", t=PACK, i=4),
                 in_=o_f32[h][:].rearrange("p t (c i) -> p c t i", i=4),
             )
-        for h in range(HALVES):
-            cols = slice(h * P, (h + 1) * P)
-            nc.vector.quantize_mx(out=out_codes[:, cols].bitcast(FP8X4), scales=out_scales[:, cols], in_=o_bf[h][:])
-        nc.scalar.dma_start(
-            out=out_1[0].rearrange("p n t -> p (n t)").bitcast(I32),
-            in_=out_codes[:].bitcast(I32),
-        )
+            nc.vector.quantize_mx(out=out_codes[:, cols].bitcast(FP8X4), scales=out_scales[:, cols], in_=o_bf[:])
+            nc.sync.dma_start(
+                out=out_1[0].rearrange("p n t -> p (n t)").bitcast(I32)[:, cols],
+                in_=out_codes[:, cols].bitcast(I32),
+            )
         for q in range(4):
-            queue = nc.sync if q < 2 else nc.scalar
+            queue = nc.sync if q < 1 else nc.scalar
             queue.dma_start(
                 out=out_2[0, 4 * q : 4 * q + 4, :].bitcast(I32),
                 in_=out_scales[32 * q : 32 * q + 4, :].bitcast(I32),

@@ -97,11 +97,10 @@ def tile_picked_zbloom_none_po_kernel(
         nc.gpsimd.memset(x_sc[:].bitcast(I32), 0)
         for j in range(4):
             nc.sync.dma_start(out=x_sc[j:P:32, :].bitcast(I32), in_=picked_sc[8 * j : P : 32, :].bitcast(I32))
-        w2_both = tile([P, 2, PACK, HALF], F32, "w2_both", "w2_raw0")
-        w2_raw = [w2_both[:, part] for part in range(2)]
+        w2_raw = tile([P, 2, PACK, HALF], F32, "w2_raw", "w2_raw0")
         for part in range(2):
             nc.sync.dma_start(
-                out=w2_raw[part], in_=w2.rearrange("(p j) c -> p j c", j=PACK)[:, :, part * HALF : (part + 1) * HALF]
+                out=w2_raw[:, part], in_=w2.rearrange("(p j) c -> p j c", j=PACK)[:, :, part * HALF : (part + 1) * HALF]
             )
         x_w = []
         for a in range(2):
@@ -110,7 +109,7 @@ def tile_picked_zbloom_none_po_kernel(
             x_w.append(picked)
 
         warm = bank(7, [P, HALF], "warm")
-        for turn in range(5):
+        for turn in range(4):
             nc.tensor.matmul_mx(
                 out=warm[:],
                 lhsT=w1_mx[0][0][:, :P].bitcast(FP8X4),
@@ -119,12 +118,6 @@ def tile_picked_zbloom_none_po_kernel(
                 rhs_scale=w1_mx[0][1][:],
                 start=True,
                 stop=True,
-            )
-
-        def deal(copy, rounded, raw, lo, hi, at):
-            copy(
-                out=rounded[:, :, at + lo : at + hi, :].rearrange("p t q j -> p q j t"),
-                in_=raw.rearrange("p j (q t) -> p q j t", t=PACK)[:, lo:hi],
             )
 
         w1_mx.append(quantise_w1(1, round_w1(1)))
@@ -213,18 +206,21 @@ def tile_picked_zbloom_none_po_kernel(
                 z_pairs[:, u, :], z_rows[:, u].rearrange("p q e -> p (q e)").bitcast(F32), ident[:]
             )
 
-        w2_codes = tile([P, N], U32, "w2_codes", "chain11")
-        w2_scales = tile([P, N], U8, "w2_scales")
-        for part in range(2):
-            rounded = tile([P, PACK, Q, PACK], BF16, "w2_bf%d" % part, ("w1_bf1", "gate_last")[part])
-            deal((nc.vector.tensor_copy, nc.scalar.copy)[part], rounded, w2_raw[part], 0, Q, 0)
-            for t in range(PACK):
-                cols = slice(t * P + part * Q, t * P + (part + 1) * Q)
-                nc.vector.quantize_mx(
-                    out=w2_codes[:, cols].bitcast(FP8X4),
-                    scales=w2_scales[:, cols],
-                    in_=rounded[:, t].rearrange("p q j -> p (q j)"),
+        w2_mx = []
+        for pair in range(2):
+            rounded = tile([P, 2, P, PACK], BF16, "w2_bf%d" % pair, ("w1_bf1", "gate_last")[pair])
+            copy = (nc.vector.tensor_copy, nc.scalar.copy)[pair]
+            for part in range(2):
+                copy(
+                    out=rounded[:].rearrange("p e m j -> p m j e")[:, part * Q : (part + 1) * Q],
+                    in_=w2_raw[:, part].rearrange("p j (m u e) -> p u m j e", u=2, e=2)[:, pair],
                 )
+            codes = tile([P, HALF], U32, "w2_codes%d" % pair)
+            scales = tile([P, HALF], U8, "w2_scales%d" % pair)
+            nc.vector.quantize_mx(
+                out=codes[:].bitcast(FP8X4), scales=scales[:], in_=rounded[:].rearrange("p e m j -> p (e m j)")
+            )
+            w2_mx.append((codes, scales))
 
         z_codes = tile([P, V], U32, "z_codes")
         z_scales = tile([P, V], U8, "z_scales")
@@ -253,11 +249,10 @@ def tile_picked_zbloom_none_po_kernel(
             for pair in range(2):
                 o_ps = bank(2 + 2 * h + pair, [P, 2, P], "o_ps%d%d" % (h, pair))
                 for e in range(2):
-                    t = 2 * pair + e
                     nc.tensor.matmul_mx(
                         out=o_ps[:, e, :],
-                        lhsT=w2_codes[:, t * P : (t + 1) * P].bitcast(FP8X4),
-                        lhsT_scale=w2_scales[:, t * P : (t + 1) * P],
+                        lhsT=w2_mx[pair][0][:, e * P : (e + 1) * P].bitcast(FP8X4),
+                        lhsT_scale=w2_mx[pair][1][:, e * P : (e + 1) * P],
                         rhs=z_codes[:, cols].bitcast(FP8X4),
                         rhs_scale=z_scales[:, cols],
                         start=True,

@@ -97,11 +97,8 @@ def tile_picked_zbloom_none_po_kernel(
         nc.gpsimd.memset(x_sc[:].bitcast(I32), 0)
         for j in range(4):
             nc.sync.dma_start(out=x_sc[j:P:32, :].bitcast(I32), in_=picked_sc[8 * j : P : 32, :].bitcast(I32))
-        w2_raw = tile([P, 2, PACK, HALF], F32, "w2_raw", "w2_raw0")
-        for part in range(2):
-            nc.sync.dma_start(
-                out=w2_raw[:, part], in_=w2.rearrange("(p j) c -> p j c", j=PACK)[:, :, part * HALF : (part + 1) * HALF]
-            )
+        w2_raw = tile([P, PACK, N], F32, "w2_raw", "w2_raw0")
+        nc.sync.dma_start(out=w2_raw[:], in_=w2.rearrange("(p j) c -> p j c", j=PACK))
         x_w = []
         for a in range(2):
             picked = tile([P, S // 2], U32, "x_w%d" % a)
@@ -210,10 +207,10 @@ def tile_picked_zbloom_none_po_kernel(
         for pair in range(2):
             rounded = tile([P, 2, P, PACK], BF16, "w2_bf%d" % pair, ("w1_bf1", "gate_last")[pair])
             copy = (nc.vector.tensor_copy, nc.scalar.copy)[pair]
-            for part in range(2):
+            for lo, hi in ((0, Q), (Q, P)) if pair == 0 else ((0, P),):
                 copy(
-                    out=rounded[:].rearrange("p e m j -> p m j e")[:, part * Q : (part + 1) * Q],
-                    in_=w2_raw[:, part].rearrange("p j (m u e) -> p u m j e", u=2, e=2)[:, pair],
+                    out=rounded[:].rearrange("p e m j -> p m j e")[:, lo:hi],
+                    in_=w2_raw[:].rearrange("p j (m u e) -> p u m j e", u=2, e=2)[:, pair, lo:hi],
                 )
             codes = tile([P, HALF], U32, "w2_codes%d" % pair)
             scales = tile([P, HALF], U8, "w2_scales%d" % pair)

@@ -239,10 +239,9 @@ def tile_picked_zbloom_none_po_kernel(
         out_codes = tile([P, V], U32, "out_codes")
         out_scales = tile([P, V], U8, "out_scales")
         out_view = out_0.rearrange("(p t) v -> p t v", t=PACK)
-        o_f32 = []
+        o_f32 = tile([P, PACK, V], F32, "o_f32")
         for h in range(HALVES):
             cols = slice(h * P, (h + 1) * P)
-            o_f32.append(tile([P, PACK, P], F32, "o_f32%d" % h))
             for pair in range(2):
                 o_ps = bank(2 + 2 * h + pair, [P, 2, P], "o_ps%d%d" % (h, pair))
                 for e in range(2):
@@ -256,12 +255,14 @@ def tile_picked_zbloom_none_po_kernel(
                         stop=True,
                     )
                 copy = nc.vector.tensor_copy if (h, pair) == (0, 1) else nc.scalar.copy
-                copy(out=o_f32[h][:, 2 * pair : 2 * pair + 2, :], in_=o_ps[:])
-            nc.sync.dma_start(out=out_view[:, :, cols], in_=o_f32[h][:])
+                rows = slice(2 * pair, 2 * pair + 2)
+                copy(out=o_f32[:, rows, cols], in_=o_ps[:])
+                if h == HALVES - 1:
+                    nc.sync.dma_start(out=out_view[:, rows, :], in_=o_f32[:, rows, :])
             o_bf = tile([P, P * PACK], BF16, "o_bf%d" % h)
             nc.vector.tensor_copy(
                 out=o_bf[:].rearrange("p (c i t) -> p c t i", t=PACK, i=4),
-                in_=o_f32[h][:].rearrange("p t (c i) -> p c t i", i=4),
+                in_=o_f32[:, :, cols].rearrange("p t (c i) -> p c t i", i=4),
             )
             nc.vector.quantize_mx(out=out_codes[:, cols].bitcast(FP8X4), scales=out_scales[:, cols], in_=o_bf[:])
             nc.sync.dma_start(

@@ -260,17 +260,19 @@ def tile_picked_zbloom_none_po_kernel(
                 if h == HALVES - 1:
                     nc.sync.dma_start(out=out_view[:, rows, :], in_=o_f32[:, rows, :])
             o_bf = tile([P, P * PACK], BF16, "o_bf%d" % h)
-            nc.vector.tensor_copy(
-                out=o_bf[:].rearrange("p (c i t) -> p c t i", t=PACK, i=4),
-                in_=o_f32[:, :, cols].rearrange("p t (c i) -> p c t i", i=4),
-            )
+            own = (P // 4, 20)[h]
+            for copy, lo, hi in ((nc.vector.tensor_copy, 0, own), (nc.scalar.copy, own, P // 4))[: h + 1]:
+                copy(
+                    out=o_bf[:].rearrange("p (c i t) -> p c t i", t=PACK, i=4)[:, lo:hi],
+                    in_=o_f32[:, :, cols].rearrange("p t (c i) -> p c t i", i=4)[:, lo:hi],
+                )
             nc.vector.quantize_mx(out=out_codes[:, cols].bitcast(FP8X4), scales=out_scales[:, cols], in_=o_bf[:])
-            nc.sync.dma_start(
+            nc.scalar.dma_start(
                 out=out_1[0].rearrange("p n t -> p (n t)").bitcast(I32)[:, cols],
                 in_=out_codes[:, cols].bitcast(I32),
             )
         for q in range(4):
-            queue = nc.sync if q < 1 else nc.scalar
+            queue = nc.sync if q < 3 else nc.scalar
             queue.dma_start(
                 out=out_2[0, 4 * q : 4 * q + 4, :].bitcast(I32),
                 in_=out_scales[32 * q : 32 * q + 4, :].bitcast(I32),

@@ -39,19 +39,19 @@ def tile_picked_zbloom_none_po_kernel(
         def tile(shape, dtype, name, tag=None):
             return sb.tile(shape, dtype, name=name, tag=tag or name, align_bytes=64)
 
-        gate_rows = tile([P, V], F32, "gate_rows")
-        nc.gpsimd.memset(gate_rows[:], 0.0)
-        scale_table = tile([P, T], U8, "scale_table", "w2_raw0")
+        scale_table = tile([P, T], U8, "scale_table", "w2_raw")
         nc.gpsimd.memset(scale_table[:, : T // 2].bitcast(I32), 0)
         nc.vector.memset(scale_table[:, T // 2 :].bitcast(I32), 0)
+        gate_rows = tile([P, V], F32, "gate_rows")
+        nc.gpsimd.memset(gate_rows[:], 0.0)
 
-        def load_half(weight, part, name):
-            raw = tile([P, PACK, HALF], F32, name)
-            view = weight.rearrange("(p j) c -> p j c", j=PACK)
+        def load_half(part):
+            raw = tile([P, PACK, HALF], F32, "w1_raw%d" % part)
+            view = w1.rearrange("(p j) c -> p j c", j=PACK)
             nc.sync.dma_start(out=raw[:], in_=view[:, :, part * HALF : (part + 1) * HALF])
             return raw
 
-        w1_raw = [load_half(w1, 0, "w1_raw0")]
+        w1_raw = [load_half(0)]
         offsets = sb.tile([P, S // 16], U16, name="offsets")
         nc.sync.dma_start(offsets[:], offs)
         nc.sync.dma_start(out=scale_table[0:P:8, :].bitcast(I32), in_=x_scales[0].bitcast(I32))
@@ -61,7 +61,7 @@ def tile_picked_zbloom_none_po_kernel(
         nc.sync.dma_start(out=word_table[:, :first].bitcast(I32), in_=words_in[:, :first])
         nc.sync.dma_start(out=gate_rows[0:D, :], in_=gate[:, 0, :])
         nc.sync.dma_start(out=word_table[:, first:].bitcast(I32), in_=words_in[:, first:])
-        w1_raw.append(load_half(w1, 1, "w1_raw1"))
+        w1_raw.append(load_half(1))
 
         ident = tile([P, P], F32, "ident")
         make_identity(nc, ident[:])
@@ -69,8 +69,8 @@ def tile_picked_zbloom_none_po_kernel(
         def round_w1(part):
             rounded = tile([P, HALF * PACK], BF16, "w1_bf%d" % part)
             nc.scalar.copy(
-                out=rounded[:].rearrange("p (q t j) -> p q j t", t=PACK, j=PACK),
-                in_=w1_raw[part][:].rearrange("p j (q t) -> p q j t", t=PACK),
+                out=rounded[:].rearrange("p (u q e j) -> p q j u e", u=2, e=2, j=PACK),
+                in_=w1_raw[part][:].rearrange("p j (q u e) -> p q j u e", u=2, e=2),
             )
             return rounded
 
@@ -87,8 +87,6 @@ def tile_picked_zbloom_none_po_kernel(
             nc.tensor.transpose(gate_ps[:, h, :], gate_rows[:, h * P : (h + 1) * P], ident[:])
         gate_col = tile([P, HALVES, D], F32, "gate_col")
         nc.scalar.activation(gate_col[:], gate_ps[:, :, 0:D], COPY)
-        gate_last = tile([P, 1], F32, "gate_last")
-        nc.scalar.activation(gate_last[:], gate_ps[:, 0, D - 1 : D], COPY)
 
         picked_sc = tile([P, S], U8, "picked_sc")
         nc.vector.tensor_copy(picked_sc[:], scale_table[:].indirect(offsets[:]))
@@ -97,16 +95,16 @@ def tile_picked_zbloom_none_po_kernel(
         nc.gpsimd.memset(x_sc[:].bitcast(I32), 0)
         for j in range(4):
             nc.sync.dma_start(out=x_sc[j:P:32, :].bitcast(I32), in_=picked_sc[8 * j : P : 32, :].bitcast(I32))
-        w2_raw = tile([P, PACK, N], F32, "w2_raw", "w2_raw0")
+        w2_raw = tile([P, PACK, N], F32, "w2_raw")
         nc.sync.dma_start(out=w2_raw[:], in_=w2.rearrange("(p j) c -> p j c", j=PACK))
         x_w = []
-        for a in range(2):
-            picked = tile([P, S // 2], U32, "x_w%d" % a)
-            nc.vector.tensor_copy(picked[:], word_table[:].indirect(offsets[:, a * 32 : (a + 1) * 32]))
+        for d in range(D):
+            picked = tile([P, V], U32, "x_w%d" % d)
+            nc.vector.tensor_copy(picked[:], word_table[:].indirect(offsets[:, d * 16 : (d + 1) * 16]))
             x_w.append(picked)
 
         warm = bank(7, [P, HALF], "warm")
-        for turn in range(4):
+        for turn in range(2):
             nc.tensor.matmul_mx(
                 out=warm[:],
                 lhsT=w1_mx[0][0][:, :P].bitcast(FP8X4),
@@ -120,98 +118,83 @@ def tile_picked_zbloom_none_po_kernel(
         w1_mx.append(quantise_w1(1, round_w1(1)))
 
         y = {}
+        for part in range(2):
+            for d in range(D):
+                for h in range(HALVES):
+                    if d % 2 == 0:
+                        both = bank(4 * part + d + h, [P, 2, HALF], "y%d%d%d" % (part, d, h))
+                        y[d, h, part], y[d + 1, h, part] = both[:, 0, :], both[:, 1, :]
+                    nc.tensor.matmul_mx(
+                        out=y[d, h, part],
+                        lhsT=x_w[d][:, h * P : (h + 1) * P].bitcast(FP8X4),
+                        lhsT_scale=x_sc[:, d * V + h * P : d * V + (h + 1) * P],
+                        rhs=w1_mx[part][0][:].bitcast(FP8X4),
+                        rhs_scale=w1_mx[part][1][:],
+                        start=True,
+                        stop=True,
+                    )
 
-        def first_product(d, h, part):
-            codes, scales = w1_mx[part]
-            at = d * V + h * P
-            local = at % (S // 2)
-            nc.tensor.matmul_mx(
-                out=y[d, h, part],
-                lhsT=x_w[d // 2][:, local : local + P].bitcast(FP8X4),
-                lhsT_scale=x_sc[:, at : at + P],
-                rhs=codes[:].bitcast(FP8X4),
-                rhs_scale=scales[:],
-                start=True,
-                stop=True,
-            )
-
-        terms = [tile([P, PACK, P], F32, "term%d" % d) for d in range(D)]
-        z_rows = tile([P, 2, P, 2], BF16, "z_rows")
+        terms = [tile([P, 2, 2, P], F32, "term%d" % d) for d in range(D)]
+        gate_last = tile([P, 1], F32, "gate_last")
+        nc.scalar.activation(gate_last[:], gate_col[:, 0, D - 1 : D], COPY)
+        z_rows = tile([P, 2, HALF], BF16, "z_rows")
         acc = {}
-
-        def scale_first(part):
-            acc[part] = tile([P, HALF], F32, "acc%d" % part)
-            nc.vector.tensor_scalar(acc[part][:], y[0, 1, part], gate_col[:, 1, 0:1], None, MULT)
 
         def own_term(d, part):
             nc.scalar.activation(
-                terms[d][:, :, part * Q : (part + 1) * Q],
-                y[d, 0, part].rearrange("p (q t) -> p t q", t=PACK),
+                terms[d][:, :, :, part * Q : (part + 1) * Q],
+                y[d, 0, part].rearrange("p (u q e) -> p u e q", u=2, e=2),
                 COPY,
                 scale=gate_last[:] if d == D - 1 else gate_col[:, 0, d : d + 1],
             )
 
         def chain(d, part):
-            nxt = tile([P, HALF], F32, "chain%d%d" % (d, part))
-            nc.vector.scalar_tensor_tensor(nxt[:], y[d, 1, part], gate_col[:, 1, d : d + 1], acc[part][:], MULT, ADD)
-            acc[part] = nxt
-
-        def chain_end(part):
-            for u in range(2):
+            gate_d = gate_col[:, 1, d : d + 1]
+            if d == D - 1:
                 nc.vector.scalar_tensor_tensor(
-                    z_rows[:, u, part * Q : (part + 1) * Q, :],
-                    y[3, 1, part].rearrange("p (q u e) -> p u q e", u=2, e=2)[:, u],
-                    gate_col[:, 1, 3:4],
-                    acc[part][:].rearrange("p (q u e) -> p u q e", u=2, e=2)[:, u],
+                    z_rows[:, :, part * P : (part + 1) * P],
+                    y[d, 1, part].rearrange("p (u c) -> p u c", u=2),
+                    gate_d,
+                    acc[part][:].rearrange("p (u c) -> p u c", u=2),
                     MULT,
                     ADD,
                 )
+                return
+            nxt = tile([P, HALF], F32, "acc%d%d" % (d, part))
+            if d == 0:
+                nc.vector.tensor_scalar(nxt[:], y[d, 1, part], gate_d, None, MULT)
+            else:
+                nc.vector.scalar_tensor_tensor(nxt[:], y[d, 1, part], gate_d, acc[part][:], MULT, ADD)
+            acc[part] = nxt
 
-        for part in range(2):
-            for pair in range(2):
-                for h in range(HALVES):
-                    both = bank(4 * part + 2 * pair + h, [P, 2, HALF], "y%d%d%d" % (part, pair, h))
-                    for e in range(2):
-                        y[2 * pair + e, h, part] = both[:, e, :]
-                        first_product(2 * pair + e, h, part)
         for part in range(2):
             for d in range(D):
                 own_term(d, part)
-        scale_first(0)
-        chain(1, 0)
-        scale_first(1)
-        chain(2, 0)
-        chain(1, 1)
-        chain_end(0)
-        chain(2, 1)
-        chain_end(1)
+        for d, part in ((0, 0), (1, 0), (0, 1), (2, 0), (1, 1), (3, 0), (2, 1), (3, 1)):
+            chain(d, part)
 
         z_sum = bank(0, [P, PACK, P], "z_sum")
-        for d in range(D):
+        for n, term in enumerate(terms):
             for t in range(PACK):
                 nc.tensor.matmul(
                     z_sum[:, t, :],
-                    lhsT=terms[d][:, t, :],
+                    lhsT=term[:, t // 2, t % 2, :],
                     rhs=ident[:],
                     is_transpose=True,
-                    start=(d == 0 and t == 0),
-                    stop=(d == D - 1 and t == PACK - 1),
+                    start=(n == 0 and t == 0),
+                    stop=(n == len(terms) - 1 and t == PACK - 1),
                 )
         z_pairs = bank(1, [P, 2, P], "z_pairs")
         for u in range(2):
-            nc.tensor.transpose(
-                z_pairs[:, u, :], z_rows[:, u].rearrange("p q e -> p (q e)").bitcast(F32), ident[:]
-            )
+            nc.tensor.transpose(z_pairs[:, u, :], z_rows[:, u, :].bitcast(F32), ident[:])
 
         w2_mx = []
         for pair in range(2):
             rounded = tile([P, 2, P, PACK], BF16, "w2_bf%d" % pair, ("w1_bf1", "gate_last")[pair])
+            source = w2_raw[:].rearrange("p j (m u e) -> p u m j e", u=2, e=2)[:, pair]
             copy = (nc.vector.tensor_copy, nc.scalar.copy)[pair]
             for lo, hi in ((0, Q), (Q, P)) if pair == 0 else ((0, P),):
-                copy(
-                    out=rounded[:].rearrange("p e m j -> p m j e")[:, lo:hi],
-                    in_=w2_raw[:].rearrange("p j (m u e) -> p u m j e", u=2, e=2)[:, pair, lo:hi],
-                )
+                copy(out=rounded[:].rearrange("p e m j -> p m j e")[:, lo:hi], in_=source[:, lo:hi])
             codes = tile([P, HALF], U32, "w2_codes%d" % pair)
             scales = tile([P, HALF], U8, "w2_scales%d" % pair)
             nc.vector.quantize_mx(

@@ -118,35 +118,52 @@ def tile_picked_zbloom_none_po_kernel(
         w1_mx.append(quantise_w1(1, round_w1(1)))
 
         y = {}
-        for part in range(2):
-            for d in range(D):
-                for h in range(HALVES):
-                    if d % 2 == 0:
-                        both = bank(4 * part + d + h, [P, 2, HALF], "y%d%d%d" % (part, d, h))
-                        y[d, h, part], y[d + 1, h, part] = both[:, 0, :], both[:, 1, :]
-                    nc.tensor.matmul_mx(
-                        out=y[d, h, part],
-                        lhsT=x_w[d][:, h * P : (h + 1) * P].bitcast(FP8X4),
-                        lhsT_scale=x_sc[:, d * V + h * P : d * V + (h + 1) * P],
-                        rhs=w1_mx[part][0][:].bitcast(FP8X4),
-                        rhs_scale=w1_mx[part][1][:],
-                        start=True,
-                        stop=True,
-                    )
+        by_hash = (((0, 1), (0, 0)), ((1, 1), (2, 1)), ((1, 0), (2, 0)), ((3, 0), (3, 1)))
+        by_need = (((0, 1), (1, 0)), ((1, 1), (3, 0)), ((0, 0), (2, 0)), ((2, 1), (3, 1)))
+        for part, shares in enumerate((by_hash, by_need)):
+            for n, pieces in enumerate(shares):
+                both = bank(4 * part + n, [P, 2, HALF], "y%d%d" % (part, n))
+                for e, (d, h) in enumerate(pieces):
+                    y[d, h, part] = both[:, e, :]
+            for d, h in (piece for pieces in shares for piece in pieces):
+                nc.tensor.matmul_mx(
+                    out=y[d, h, part],
+                    lhsT=x_w[d][:, h * P : (h + 1) * P].bitcast(FP8X4),
+                    lhsT_scale=x_sc[:, d * V + h * P : d * V + (h + 1) * P],
+                    rhs=w1_mx[part][0][:].bitcast(FP8X4),
+                    rhs_scale=w1_mx[part][1][:],
+                    start=True,
+                    stop=True,
+                )
 
         terms = [tile([P, 2, 2, P], F32, "term%d" % d) for d in range(D)]
-        gate_last = tile([P, 1], F32, "gate_last")
-        nc.scalar.activation(gate_last[:], gate_col[:, 0, D - 1 : D], COPY)
+        w2_bf = [tile([P, 2 * P * PACK], BF16, "w2_bf%d" % pair) for pair in range(2)]
+        gate_last = w2_bf[1][:, 2 * P * PACK - 2 :].bitcast(F32)
+        nc.scalar.activation(gate_last, gate_col[:, 0, 2:3], COPY)
         z_rows = tile([P, 2, HALF], BF16, "z_rows")
         acc = {}
+
+        def planes(d, part):
+            return y[d, 0, part].rearrange("p (u q e) -> p u e q", u=2, e=2)
 
         def own_term(d, part):
             nc.scalar.activation(
                 terms[d][:, :, :, part * Q : (part + 1) * Q],
-                y[d, 0, part].rearrange("p (u q e) -> p u e q", u=2, e=2),
+                planes(d, part),
                 COPY,
-                scale=gate_last[:] if d == D - 1 else gate_col[:, 0, d : d + 1],
+                scale=gate_last if d == 2 else gate_col[:, 0, d : d + 1],
             )
+
+        def seed(part):
+            acc[part] = tile([P, HALF], F32, "seed%d" % part)
+            nc.scalar.activation(acc[part][:], y[0, 1, part], COPY, scale=gate_col[:, 1, 0:1])
+
+        def joined_term(part):
+            for u in range(2):
+                places = slice(part * Q, (part + 1) * Q)
+                nc.vector.scalar_tensor_tensor(
+                    terms[3][:, u, :, places], planes(3, part)[:, u], gate_col[:, 0, 3:4], terms[1][:, u, :, places], MULT, ADD
+                )
 
         def chain(d, part):
             gate_d = gate_col[:, 1, d : d + 1]
@@ -161,17 +178,18 @@ def tile_picked_zbloom_none_po_kernel(
                 )
                 return
             nxt = tile([P, HALF], F32, "acc%d%d" % (d, part))
-            if d == 0:
-                nc.vector.tensor_scalar(nxt[:], y[d, 1, part], gate_d, None, MULT)
-            else:
-                nc.vector.scalar_tensor_tensor(nxt[:], y[d, 1, part], gate_d, acc[part][:], MULT, ADD)
+            nc.vector.scalar_tensor_tensor(nxt[:], y[d, 1, part], gate_d, acc[part][:], MULT, ADD)
             acc[part] = nxt
 
         for part in range(2):
-            for d in range(D):
+            seed(part)
+            for d in ((0, 1, 2), (1, 0, 2))[part]:
                 own_term(d, part)
-        for d, part in ((0, 0), (1, 0), (0, 1), (2, 0), (1, 1), (3, 0), (2, 1), (3, 1)):
-            chain(d, part)
+            chain(1, part)
+            joined_term(part)
+            chain(2, part)
+            chain(3, part)
+        terms = (terms[0], terms[3], terms[2])
 
         z_sum = bank(0, [P, PACK, P], "z_sum")
         for n, term in enumerate(terms):
@@ -184,21 +202,29 @@ def tile_picked_zbloom_none_po_kernel(
                     start=(n == 0 and t == 0),
                     stop=(n == len(terms) - 1 and t == PACK - 1),
                 )
-        z_pairs = bank(1, [P, 2, P], "z_pairs")
+        z_pairs = bank(6, [P, 2, P], "z_pairs")
         for u in range(2):
             nc.tensor.transpose(z_pairs[:, u, :], z_rows[:, u, :].bitcast(F32), ident[:])
 
         w2_mx = []
         for pair in range(2):
-            rounded = tile([P, 2, P, PACK], BF16, "w2_bf%d" % pair, ("w1_bf1", "gate_last")[pair])
+            rounded = w2_bf[pair][:].rearrange("p (e m j) -> p e m j", e=2, j=PACK)
             source = w2_raw[:].rearrange("p j (m u e) -> p u m j e", u=2, e=2)[:, pair]
-            copy = (nc.vector.tensor_copy, nc.scalar.copy)[pair]
-            for lo, hi in ((0, Q), (Q, P)) if pair == 0 else ((0, P),):
-                copy(out=rounded[:].rearrange("p e m j -> p m j e")[:, lo:hi], in_=source[:, lo:hi])
+            own = (P, Q)[pair]
+            nc.gpsimd.tensor_scalar(
+                rounded.rearrange("p e m j -> p m e j")[:, :own],
+                source.rearrange("p m j e -> p m e j")[:, :own],
+                1.0,
+                0.0,
+                MULT,
+                ADD,
+            )
+            if pair == 1:
+                nc.scalar.copy(out=rounded.rearrange("p e m j -> p m j e")[:, own:], in_=source[:, own:])
             codes = tile([P, HALF], U32, "w2_codes%d" % pair)
             scales = tile([P, HALF], U8, "w2_scales%d" % pair)
             nc.vector.quantize_mx(
-                out=codes[:].bitcast(FP8X4), scales=scales[:], in_=rounded[:].rearrange("p e m j -> p (e m j)")
+                out=codes[:].bitcast(FP8X4), scales=scales[:], in_=w2_bf[pair][:]
             )
             w2_mx.append((codes, scales))
 
@@ -213,7 +239,7 @@ def tile_picked_zbloom_none_po_kernel(
                     in_=z_sum[:].rearrange("p t v -> p v t"),
                 )
             else:
-                nc.scalar.copy(
+                nc.vector.tensor_copy(
                     out=z_bf[:].bitcast(F32).rearrange("p (v u) -> p v u", u=2),
                     in_=z_pairs[:].rearrange("p u v -> p v u"),
                 )

@@ -88,6 +88,10 @@ def tile_picked_zbloom_none_po_kernel(
         gate_col = tile([P, HALVES, D], F32, "gate_col")
         nc.scalar.activation(gate_col[:], gate_ps[:, :, 0:D], COPY)
 
+        w2_bf = [tile([P, 2 * P * PACK], BF16, "w2_bf%d" % pair) for pair in range(2)]
+        gate_last = w2_bf[1][:, 2 * P * PACK - 2 :].bitcast(F32)
+        nc.scalar.activation(gate_last, gate_ps[:, 0, 2:3], COPY)
+
         picked_sc = tile([P, S], U8, "picked_sc")
         nc.vector.tensor_copy(picked_sc[:], scale_table[:].indirect(offsets[:]))
         w1_mx = [quantise_w1(0, w1_first)]
@@ -98,13 +102,13 @@ def tile_picked_zbloom_none_po_kernel(
         w2_raw = tile([P, PACK, N], F32, "w2_raw")
         nc.sync.dma_start(out=w2_raw[:], in_=w2.rearrange("(p j) c -> p j c", j=PACK))
         x_w = []
-        for d in range(D):
-            picked = tile([P, V], U32, "x_w%d" % d)
-            nc.vector.tensor_copy(picked[:], word_table[:].indirect(offsets[:, d * 16 : (d + 1) * 16]))
-            x_w.append(picked)
+        for a in range(2):
+            picked = tile([P, S // 2], U32, "x_w%d" % a)
+            nc.vector.tensor_copy(picked[:], word_table[:].indirect(offsets[:, a * 32 : (a + 1) * 32]))
+            x_w.extend([picked[:, :V], picked[:, V:]])
 
         warm = bank(7, [P, HALF], "warm")
-        for turn in range(2):
+        for turn in range(4):
             nc.tensor.matmul_mx(
                 out=warm[:],
                 lhsT=w1_mx[0][0][:, :P].bitcast(FP8X4),
@@ -118,14 +122,16 @@ def tile_picked_zbloom_none_po_kernel(
         w1_mx.append(quantise_w1(1, round_w1(1)))
 
         y = {}
-        by_hash = (((0, 1), (0, 0)), ((1, 1), (2, 1)), ((1, 0), (2, 0)), ((3, 0), (3, 1)))
-        by_need = (((0, 1), (1, 0)), ((1, 1), (3, 0)), ((0, 0), (2, 0)), ((2, 1), (3, 1)))
-        for part, shares in enumerate((by_hash, by_need)):
-            for n, pieces in enumerate(shares):
-                both = bank(4 * part + n, [P, 2, HALF], "y%d%d" % (part, n))
+        shares = (
+            ((0, ((0, 1), (1, 0))), (1, ((1, 1),)), (2, ((0, 0),)), (3, ((3, 0), (2, 1))), (4, ((2, 0),)), (5, ((3, 1),))),
+            ((6, ((0, 1), (1, 0))), (7, ((1, 1), (3, 0))), (0, ((0, 0), (2, 0))), (1, ((2, 1), (3, 1)))),
+        )
+        for part in range(2):
+            for b, pieces in shares[part]:
+                held = bank(b, [P, len(pieces), HALF], "y%d%d" % (part, b))
                 for e, (d, h) in enumerate(pieces):
-                    y[d, h, part] = both[:, e, :]
-            for d, h in (piece for pieces in shares for piece in pieces):
+                    y[d, h, part] = held[:, e, :]
+            for d, h in (piece for b, pieces in shares[part] for piece in pieces):
                 nc.tensor.matmul_mx(
                     out=y[d, h, part],
                     lhsT=x_w[d][:, h * P : (h + 1) * P].bitcast(FP8X4),
@@ -137,9 +143,6 @@ def tile_picked_zbloom_none_po_kernel(
                 )
 
         terms = [tile([P, 2, 2, P], F32, "term%d" % d) for d in range(D)]
-        w2_bf = [tile([P, 2 * P * PACK], BF16, "w2_bf%d" % pair) for pair in range(2)]
-        gate_last = w2_bf[1][:, 2 * P * PACK - 2 :].bitcast(F32)
-        nc.scalar.activation(gate_last, gate_col[:, 0, 2:3], COPY)
         z_rows = tile([P, 2, HALF], BF16, "z_rows")
         acc = {}
 
@@ -183,7 +186,7 @@ def tile_picked_zbloom_none_po_kernel(
 
         for part in range(2):
             seed(part)
-            for d in ((0, 1, 2), (1, 0, 2))[part]:
+            for d in (1, 0, 2):
                 own_term(d, part)
             chain(1, part)
             joined_term(part)
@@ -191,7 +194,7 @@ def tile_picked_zbloom_none_po_kernel(
             chain(3, part)
         terms = (terms[0], terms[3], terms[2])
 
-        z_sum = bank(0, [P, PACK, P], "z_sum")
+        z_sum = bank(2, [P, PACK, P], "z_sum")
         for n, term in enumerate(terms):
             for t in range(PACK):
                 nc.tensor.matmul(
@@ -202,7 +205,7 @@ def tile_picked_zbloom_none_po_kernel(
                     start=(n == 0 and t == 0),
                     stop=(n == len(terms) - 1 and t == PACK - 1),
                 )
-        z_pairs = bank(6, [P, 2, P], "z_pairs")
+        z_pairs = bank(0, [P, 2, P], "z_pairs")
         for u in range(2):
             nc.tensor.transpose(z_pairs[:, u, :], z_rows[:, u, :].bitcast(F32), ident[:])
 
@@ -252,7 +255,7 @@ def tile_picked_zbloom_none_po_kernel(
         for h in range(HALVES):
             cols = slice(h * P, (h + 1) * P)
             for pair in range(2):
-                o_ps = bank(2 + 2 * h + pair, [P, 2, P], "o_ps%d%d" % (h, pair))
+                o_ps = bank(3 + 2 * h + pair, [P, 2, P], "o_ps%d%d" % (h, pair))
                 for e in range(2):
                     nc.tensor.matmul_mx(
                         out=o_ps[:, e, :],

@@ -57,10 +57,8 @@ def tile_picked_zbloom_none_po_kernel(
         nc.sync.dma_start(out=scale_table[0:P:8, :].bitcast(I32), in_=x_scales[0].bitcast(I32))
         word_table = tile([P, T], U32, "word_table")
         words_in = x_words[0].rearrange("p n t -> p (n t)").bitcast(I32)
-        first = 3 * T // 4
-        nc.sync.dma_start(out=word_table[:, :first].bitcast(I32), in_=words_in[:, :first])
+        nc.sync.dma_start(out=word_table[:].bitcast(I32), in_=words_in)
         nc.sync.dma_start(out=gate_rows[0:D, :], in_=gate[:, 0, :])
-        nc.sync.dma_start(out=word_table[:, first:].bitcast(I32), in_=words_in[:, first:])
         w1_raw.append(load_half(1))
 
         ident = tile([P, P], F32, "ident")
@@ -108,7 +106,7 @@ def tile_picked_zbloom_none_po_kernel(
             x_w.extend([picked[:, :V], picked[:, V:]])
 
         warm = bank(7, [P, HALF], "warm")
-        for turn in range(4):
+        for turn in range(2):
             nc.tensor.matmul_mx(
                 out=warm[:],
                 lhsT=w1_mx[0][0][:, :P].bitcast(FP8X4),

@@ -33,33 +33,34 @@ def tile_picked_zbloom_none_po_kernel(
         sb = ctx.enter_context(tc.tile_pool(name="sb", bufs=1))
         ps = ctx.enter_context(tc.psum_pool(name="ps", bufs=1))
 
+        reused = ctx.enter_context(tc.tile_pool(name="reused", bufs=1))
+
         def bank(b, shape, name):
             return ps.tile(shape, F32, name=name, tag="bank%d" % b)
 
         def tile(shape, dtype, name, tag=None):
             return sb.tile(shape, dtype, name=name, tag=tag or name, align_bytes=64)
 
-        scale_table = tile([P, T], U8, "scale_table", "w2_raw")
+        scale_table = reused.tile([P, T], U8, name="scale_table", offset=6144)
         nc.gpsimd.memset(scale_table[:, : T // 2].bitcast(I32), 0)
         nc.vector.memset(scale_table[:, T // 2 :].bitcast(I32), 0)
         gate_rows = tile([P, V], F32, "gate_rows")
         nc.gpsimd.memset(gate_rows[:], 0.0)
 
-        def load_half(part):
-            raw = tile([P, PACK, HALF], F32, "w1_raw%d" % part)
-            view = w1.rearrange("(p j) c -> p j c", j=PACK)
-            nc.sync.dma_start(out=raw[:], in_=view[:, :, part * HALF : (part + 1) * HALF])
-            return raw
-
-        w1_raw = [load_half(0)]
+        w1_in = w1.rearrange("(p j) c -> p j c", j=PACK)
+        w1_raw = [tile([P, PACK, HALF], F32, "w1_raw0")[:]]
+        nc.sync.dma_start(out=w1_raw[0], in_=w1_in[:, :, :HALF])
         offsets = sb.tile([P, S // 16], U16, name="offsets")
         nc.sync.dma_start(offsets[:], offs)
         nc.sync.dma_start(out=scale_table[0:P:8, :].bitcast(I32), in_=x_scales[0].bitcast(I32))
         word_table = tile([P, T], U32, "word_table")
         words_in = x_words[0].rearrange("p n t -> p (n t)").bitcast(I32)
-        nc.sync.dma_start(out=word_table[:].bitcast(I32), in_=words_in)
+        first = 7 * T // 8
+        nc.sync.dma_start(out=word_table[:, :first].bitcast(I32), in_=words_in[:, :first])
         nc.sync.dma_start(out=gate_rows[0:D, :], in_=gate[:, 0, :])
-        w1_raw.append(load_half(1))
+        nc.sync.dma_start(out=word_table[:, first:].bitcast(I32), in_=words_in[:, first:])
+        late_rows = [tile([P, 2, HALF], F32, "w1_late0")[:]]
+        nc.sync.dma_start(out=late_rows[0], in_=w1_in[:, :2, HALF:])
 
         ident = tile([P, P], F32, "ident")
         make_identity(nc, ident[:])
@@ -68,7 +69,7 @@ def tile_picked_zbloom_none_po_kernel(
             rounded = tile([P, HALF * PACK], BF16, "w1_bf%d" % part)
             nc.scalar.copy(
                 out=rounded[:].rearrange("p (u q e j) -> p q j u e", u=2, e=2, j=PACK),
-                in_=w1_raw[part][:].rearrange("p j (q u e) -> p q j u e", u=2, e=2),
+                in_=w1_raw[part].rearrange("p j (q u e) -> p q j u e", u=2, e=2),
             )
             return rounded
 
@@ -94,16 +95,19 @@ def tile_picked_zbloom_none_po_kernel(
         nc.vector.tensor_copy(picked_sc[:], scale_table[:].indirect(offsets[:]))
         w1_mx = [quantise_w1(0, w1_first)]
         x_sc = tile([P, S], U8, "x_sc")
-        nc.gpsimd.memset(x_sc[:].bitcast(I32), 0)
-        for j in range(4):
+        nc.vector.tensor_copy(x_sc[:].bitcast(I32), picked_sc[:].bitcast(I32))
+        for j in range(1, 4):
             nc.sync.dma_start(out=x_sc[j:P:32, :].bitcast(I32), in_=picked_sc[8 * j : P : 32, :].bitcast(I32))
-        w2_raw = tile([P, PACK, N], F32, "w2_raw")
+        late_raw = reused.tile([P, PACK * HALF + 16], F32, name="w1_raw1", offset=10208)
+        late_rows.append(late_raw[:, : 2 * HALF].rearrange("p (j c) -> p j c", j=2))
+        nc.sync.dma_start(out=late_rows[1], in_=w1_in[:, 2:, HALF:])
+        w2_raw = reused.tile([P, PACK, N], F32, name="w2_raw", offset=0)
         nc.sync.dma_start(out=w2_raw[:], in_=w2.rearrange("(p j) c -> p j c", j=PACK))
         x_w = []
-        for a in range(2):
-            picked = tile([P, S // 2], U32, "x_w%d" % a)
-            nc.vector.tensor_copy(picked[:], word_table[:].indirect(offsets[:, a * 32 : (a + 1) * 32]))
-            x_w.extend([picked[:, :V], picked[:, V:]])
+        for lo, hi in ((0, 2), (2, 4)):
+            picked = tile([P, (hi - lo) * V], U32, "x_w%d" % lo)
+            nc.vector.tensor_copy(picked[:], word_table[:].indirect(offsets[:, lo * 16 : hi * 16]))
+            x_w.extend(picked[:, d * V : (d + 1) * V] for d in range(hi - lo))
 
         warm = bank(7, [P, HALF], "warm")
         for turn in range(2):
@@ -117,7 +121,13 @@ def tile_picked_zbloom_none_po_kernel(
                 stop=True,
             )
 
-        w1_mx.append(quantise_w1(1, round_w1(1)))
+        w1_late = tile([P, HALF * PACK], BF16, "w1_bf1")
+        for n, rows in enumerate(late_rows):
+            nc.scalar.copy(
+                out=w1_late[:].rearrange("p (u q e j) -> p q j u e", u=2, e=2, j=PACK)[:, :, 2 * n : 2 * n + 2],
+                in_=rows.rearrange("p j (q u e) -> p q j u e", u=2, e=2),
+            )
+        w1_mx.append(quantise_w1(1, w1_late))
 
         y = {}
         shares = (
@@ -129,7 +139,8 @@ def tile_picked_zbloom_none_po_kernel(
                 held = bank(b, [P, len(pieces), HALF], "y%d%d" % (part, b))
                 for e, (d, h) in enumerate(pieces):
                     y[d, h, part] = held[:, e, :]
-            for d, h in (piece for b, pieces in shares[part] for piece in pieces):
+            by_bank = [piece for b, pieces in shares[part] for piece in pieces]
+            for d, h in by_bank:
                 nc.tensor.matmul_mx(
                     out=y[d, h, part],
                     lhsT=x_w[d][:, h * P : (h + 1) * P].bitcast(FP8X4),
@@ -140,7 +151,7 @@ def tile_picked_zbloom_none_po_kernel(
                     stop=True,
                 )
 
-        terms = [tile([P, 2, 2, P], F32, "term%d" % d) for d in range(D)]
+        terms = [reused.tile([P, 2, 2, P], F32, name="term%d" % d, offset=10240 + d * H * 4) for d in range(D)]
         z_rows = tile([P, 2, HALF], BF16, "z_rows")
         acc = {}
 
@@ -156,7 +167,10 @@ def tile_picked_zbloom_none_po_kernel(
             )
 
         def seed(part):
-            acc[part] = tile([P, HALF], F32, "seed%d" % part)
+            if part == 0:
+                acc[part] = reused.tile([P, HALF], F32, name="seed0", offset=9216)
+            else:
+                acc[part] = tile([P, HALF], F32, "seed1")
             nc.scalar.activation(acc[part][:], y[0, 1, part], COPY, scale=gate_col[:, 1, 0:1])
 
         def joined_term(part):
@@ -178,7 +192,7 @@ def tile_picked_zbloom_none_po_kernel(
                     ADD,
                 )
                 return
-            nxt = tile([P, HALF], F32, "acc%d%d" % (d, part))
+            nxt = tile([P, HALF], F32, "acc%d%d" % (d, part), "w1_bf1" if (d, part) == (1, 0) else None)
             nc.vector.scalar_tensor_tensor(nxt[:], y[d, 1, part], gate_d, acc[part][:], MULT, ADD)
             acc[part] = nxt
 
@@ -211,7 +225,7 @@ def tile_picked_zbloom_none_po_kernel(
         for pair in range(2):
             rounded = w2_bf[pair][:].rearrange("p (e m j) -> p e m j", e=2, j=PACK)
             source = w2_raw[:].rearrange("p j (m u e) -> p u m j e", u=2, e=2)[:, pair]
-            own = (P, Q)[pair]
+            own = (P, P // 4)[pair]
             nc.gpsimd.tensor_scalar(
                 rounded.rearrange("p e m j -> p m e j")[:, :own],
                 source.rearrange("p m j e -> p m e j")[:, :own],

@@ -55,7 +55,7 @@ def tile_picked_zbloom_none_po_kernel(
         nc.sync.dma_start(out=scale_table[0:P:8, :].bitcast(I32), in_=x_scales[0].bitcast(I32))
         word_table = tile([P, T], U32, "word_table")
         words_in = x_words[0].rearrange("p n t -> p (n t)").bitcast(I32)
-        first = 7 * T // 8
+        first = 13 * T // 16
         nc.sync.dma_start(out=word_table[:, :first].bitcast(I32), in_=words_in[:, :first])
         nc.sync.dma_start(out=gate_rows[0:D, :], in_=gate[:, 0, :])
         nc.sync.dma_start(out=word_table[:, first:].bitcast(I32), in_=words_in[:, first:])
@@ -89,7 +89,7 @@ def tile_picked_zbloom_none_po_kernel(
 
         w2_bf = [tile([P, 2 * P * PACK], BF16, "w2_bf%d" % pair) for pair in range(2)]
         gate_last = w2_bf[1][:, 2 * P * PACK - 2 :].bitcast(F32)
-        nc.scalar.activation(gate_last, gate_ps[:, 0, 2:3], COPY)
+        nc.scalar.activation(gate_last, gate_ps[:, 0, 3:4], COPY)
 
         picked_sc = tile([P, S], U8, "picked_sc")
         nc.vector.tensor_copy(picked_sc[:], scale_table[:].indirect(offsets[:]))
@@ -130,17 +130,11 @@ def tile_picked_zbloom_none_po_kernel(
         w1_mx.append(quantise_w1(1, w1_late))
 
         y = {}
-        shares = (
-            ((0, ((0, 1), (1, 0))), (1, ((1, 1),)), (2, ((0, 0),)), (3, ((3, 0), (2, 1))), (4, ((2, 0),)), (5, ((3, 1),))),
-            ((6, ((0, 1), (1, 0))), (7, ((1, 1), (3, 0))), (0, ((0, 0), (2, 0))), (1, ((2, 1), (3, 1)))),
-        )
-        for part in range(2):
-            for b, pieces in shares[part]:
-                held = bank(b, [P, len(pieces), HALF], "y%d%d" % (part, b))
-                for e, (d, h) in enumerate(pieces):
-                    y[d, h, part] = held[:, e, :]
-            by_bank = [piece for b, pieces in shares[part] for piece in pieces]
-            for d, h in by_bank:
+        shares = (((0, 1), (0, 0)), ((1, 1), (1, 0)), ((2, 0), (3, 0)), ((2, 1), (3, 1)))
+        for part, (n, pieces) in ((part, share) for part in range(2) for share in enumerate(shares)):
+            held = bank(4 * part + n, [P, 2, HALF], "y%d%d" % (part, n))
+            for e, (d, h) in enumerate(pieces):
+                y[d, h, part] = held[:, e, :]
                 nc.tensor.matmul_mx(
                     out=y[d, h, part],
                     lhsT=x_w[d][:, h * P : (h + 1) * P].bitcast(FP8X4),
@@ -158,27 +152,19 @@ def tile_picked_zbloom_none_po_kernel(
         def planes(d, part):
             return y[d, 0, part].rearrange("p (u q e) -> p u e q", u=2, e=2)
 
-        def own_term(d, part):
+        def own_term(n, d, part):
             nc.scalar.activation(
-                terms[d][:, :, :, part * Q : (part + 1) * Q],
+                terms[n][:, :, :, part * Q : (part + 1) * Q],
                 planes(d, part),
                 COPY,
-                scale=gate_last if d == 2 else gate_col[:, 0, d : d + 1],
+                scale=gate_last if d == D - 1 else gate_col[:, 0, d : d + 1],
             )
 
-        def seed(part):
-            if part == 0:
-                acc[part] = reused.tile([P, HALF], F32, name="seed0", offset=9216)
-            else:
-                acc[part] = tile([P, HALF], F32, "seed1")
-            nc.scalar.activation(acc[part][:], y[0, 1, part], COPY, scale=gate_col[:, 1, 0:1])
-
-        def joined_term(part):
-            for u in range(2):
-                places = slice(part * Q, (part + 1) * Q)
-                nc.vector.scalar_tensor_tensor(
-                    terms[3][:, u, :, places], planes(3, part)[:, u], gate_col[:, 0, 3:4], terms[1][:, u, :, places], MULT, ADD
-                )
+        def joined_term(d, part, u):
+            places = slice(part * Q, (part + 1) * Q)
+            nc.vector.scalar_tensor_tensor(
+                terms[3][:, u, :, places], planes(d, part)[:, u], gate_col[:, 0, d : d + 1], terms[0][:, u, :, places], MULT, ADD
+            )
 
         def chain(d, part):
             gate_d = gate_col[:, 1, d : d + 1]
@@ -196,17 +182,23 @@ def tile_picked_zbloom_none_po_kernel(
             nc.vector.scalar_tensor_tensor(nxt[:], y[d, 1, part], gate_d, acc[part][:], MULT, ADD)
             acc[part] = nxt
 
+        def seed(part, into):
+            acc[part] = into
+            nc.scalar.activation(into[:], y[0, 1, part], COPY, scale=gate_col[:, 1, 0:1])
+
+        seeds = (reused.tile([P, HALF], F32, name="seed0", offset=9216), tile([P, HALF], F32, "seed1"))
         for part in range(2):
-            seed(part)
-            for d in (1, 0, 2):
-                own_term(d, part)
+            seed(part, seeds[part])
+            for n, d in ((0, 0), (1, 2), (2, 3)):
+                own_term(n, d, part)
             chain(1, part)
-            joined_term(part)
+            for u in range(2):
+                joined_term(1, part, u)
             chain(2, part)
             chain(3, part)
-        terms = (terms[0], terms[3], terms[2])
+        terms = (terms[1], terms[3], terms[2])
 
-        z_sum = bank(2, [P, PACK, P], "z_sum")
+        z_sum = bank(0, [P, PACK, P], "z_sum")
         for n, term in enumerate(terms):
             for t in range(PACK):
                 nc.tensor.matmul(
@@ -217,7 +209,7 @@ def tile_picked_zbloom_none_po_kernel(
                     start=(n == 0 and t == 0),
                     stop=(n == len(terms) - 1 and t == PACK - 1),
                 )
-        z_pairs = bank(0, [P, 2, P], "z_pairs")
+        z_pairs = bank(6, [P, 2, P], "z_pairs")
         for u in range(2):
             nc.tensor.transpose(z_pairs[:, u, :], z_rows[:, u, :].bitcast(F32), ident[:])
 
@@ -225,7 +217,7 @@ def tile_picked_zbloom_none_po_kernel(
         for pair in range(2):
             rounded = w2_bf[pair][:].rearrange("p (e m j) -> p e m j", e=2, j=PACK)
             source = w2_raw[:].rearrange("p j (m u e) -> p u m j e", u=2, e=2)[:, pair]
-            own = (P, P // 4)[pair]
+            own = (P, P // 2)[pair]
             nc.gpsimd.tensor_scalar(
                 rounded.rearrange("p e m j -> p m e j")[:, :own],
                 source.rearrange("p m j e -> p m e j")[:, :own],
@@ -254,7 +246,7 @@ def tile_picked_zbloom_none_po_kernel(
                     in_=z_sum[:].rearrange("p t v -> p v t"),
                 )
             else:
-                nc.vector.tensor_copy(
+                nc.scalar.copy(
                     out=z_bf[:].bitcast(F32).rearrange("p (v u) -> p v u", u=2),
                     in_=z_pairs[:].rearrange("p u v -> p v u"),
                 )
@@ -267,7 +259,7 @@ def tile_picked_zbloom_none_po_kernel(
         for h in range(HALVES):
             cols = slice(h * P, (h + 1) * P)
             for pair in range(2):
-                o_ps = bank(3 + 2 * h + pair, [P, 2, P], "o_ps%d%d" % (h, pair))
+                o_ps = bank(1 + 2 * h + pair, [P, 2, P], "o_ps%d%d" % (h, pair))
                 for e in range(2):
                     nc.tensor.matmul_mx(
                         out=o_ps[:, e, :],

@@ -55,7 +55,7 @@ def tile_picked_zbloom_none_po_kernel(
         nc.sync.dma_start(out=scale_table[0:P:8, :].bitcast(I32), in_=x_scales[0].bitcast(I32))
         word_table = tile([P, T], U32, "word_table")
         words_in = x_words[0].rearrange("p n t -> p (n t)").bitcast(I32)
-        first = 13 * T // 16
+        first = 7 * T // 8
         nc.sync.dma_start(out=word_table[:, :first].bitcast(I32), in_=words_in[:, :first])
         nc.sync.dma_start(out=gate_rows[0:D, :], in_=gate[:, 0, :])
         nc.sync.dma_start(out=word_table[:, first:].bitcast(I32), in_=words_in[:, first:])
@@ -87,8 +87,8 @@ def tile_picked_zbloom_none_po_kernel(
         gate_col = tile([P, HALVES, D], F32, "gate_col")
         nc.scalar.activation(gate_col[:], gate_ps[:, :, 0:D], COPY)
 
-        w2_bf = [tile([P, 2 * P * PACK], BF16, "w2_bf%d" % pair) for pair in range(2)]
-        gate_last = w2_bf[1][:, 2 * P * PACK - 2 :].bitcast(F32)
+        w2_bf = tile([P, N * PACK], BF16, "w2_bf")
+        gate_last = w2_bf[:, N * PACK - 2 :].bitcast(F32)
         nc.scalar.activation(gate_last, gate_ps[:, 0, 3:4], COPY)
 
         picked_sc = tile([P, S], U8, "picked_sc")
@@ -178,7 +178,7 @@ def tile_picked_zbloom_none_po_kernel(
                     ADD,
                 )
                 return
-            nxt = tile([P, HALF], F32, "acc%d%d" % (d, part), "w1_bf1" if (d, part) == (1, 0) else None)
+            nxt = tile([P, HALF], F32, "acc%d%d" % (d, part), {(1, 0): "w1_bf1", (1, 1): "w2_codes"}.get((d, part)))
             nc.vector.scalar_tensor_tensor(nxt[:], y[d, 1, part], gate_d, acc[part][:], MULT, ADD)
             acc[part] = nxt
 
@@ -213,27 +213,16 @@ def tile_picked_zbloom_none_po_kernel(
         for u in range(2):
             nc.tensor.transpose(z_pairs[:, u, :], z_rows[:, u, :].bitcast(F32), ident[:])
 
-        w2_mx = []
-        for pair in range(2):
-            rounded = w2_bf[pair][:].rearrange("p (e m j) -> p e m j", e=2, j=PACK)
-            source = w2_raw[:].rearrange("p j (m u e) -> p u m j e", u=2, e=2)[:, pair]
-            own = (P, P // 2)[pair]
-            nc.gpsimd.tensor_scalar(
-                rounded.rearrange("p e m j -> p m e j")[:, :own],
-                source.rearrange("p m j e -> p m e j")[:, :own],
-                1.0,
-                0.0,
-                MULT,
-                ADD,
-            )
-            if pair == 1:
-                nc.scalar.copy(out=rounded.rearrange("p e m j -> p m j e")[:, own:], in_=source[:, own:])
-            codes = tile([P, HALF], U32, "w2_codes%d" % pair)
-            scales = tile([P, HALF], U8, "w2_scales%d" % pair)
-            nc.vector.quantize_mx(
-                out=codes[:].bitcast(FP8X4), scales=scales[:], in_=w2_bf[pair][:]
-            )
-            w2_mx.append((codes, scales))
+        rounded = w2_bf[:].rearrange("p (t m j) -> p m t j", t=PACK, j=PACK)
+        source = w2_raw[:].rearrange("p j (m t) -> p m t j", t=PACK)
+        own = 88
+        nc.gpsimd.tensor_scalar(rounded[:, :own], source[:, :own], 1.0, 0.0, MULT, ADD)
+        nc.scalar.copy(
+            out=rounded[:, own:].rearrange("p m t j -> p m j t"), in_=source[:, own:].rearrange("p m t j -> p m j t")
+        )
+        w2_codes = tile([P, N], U32, "w2_codes")
+        w2_scales = tile([P, N], U8, "w2_scales")
+        nc.vector.quantize_mx(out=w2_codes[:].bitcast(FP8X4), scales=w2_scales[:], in_=w2_bf[:])
 
         z_codes = tile([P, V], U32, "z_codes")
         z_scales = tile([P, V], U8, "z_scales")
@@ -263,8 +252,8 @@ def tile_picked_zbloom_none_po_kernel(
                 for e in range(2):
                     nc.tensor.matmul_mx(
                         out=o_ps[:, e, :],
-                        lhsT=w2_mx[pair][0][:, e * P : (e + 1) * P].bitcast(FP8X4),
-                        lhsT_scale=w2_mx[pair][1][:, e * P : (e + 1) * P],
+                        lhsT=w2_codes[:, (2 * pair + e) * P : (2 * pair + e + 1) * P].bitcast(FP8X4),
+                        lhsT_scale=w2_scales[:, (2 * pair + e) * P : (2 * pair + e + 1) * P],
                         rhs=z_codes[:, cols].bitcast(FP8X4),
                         rhs_scale=z_scales[:, cols],
                         start=True,

@@ -55,7 +55,7 @@ def tile_picked_zbloom_none_po_kernel(
         nc.sync.dma_start(out=scale_table[0:P:8, :].bitcast(I32), in_=x_scales[0].bitcast(I32))
         word_table = tile([P, T], U32, "word_table")
         words_in = x_words[0].rearrange("p n t -> p (n t)").bitcast(I32)
-        first = 7 * T // 8
+        first = 3 * T // 4
         nc.sync.dma_start(out=word_table[:, :first].bitcast(I32), in_=words_in[:, :first])
         nc.sync.dma_start(out=gate_rows[0:D, :], in_=gate[:, 0, :])
         nc.sync.dma_start(out=word_table[:, first:].bitcast(I32), in_=words_in[:, first:])
@@ -89,7 +89,7 @@ def tile_picked_zbloom_none_po_kernel(
 
         w2_bf = tile([P, N * PACK], BF16, "w2_bf")
         gate_last = w2_bf[:, N * PACK - 2 :].bitcast(F32)
-        nc.scalar.activation(gate_last, gate_ps[:, 0, 3:4], COPY)
+        nc.scalar.activation(gate_last, gate_ps[:, 0, 2:3], COPY)
 
         picked_sc = tile([P, S], U8, "picked_sc")
         nc.vector.tensor_copy(picked_sc[:], scale_table[:].indirect(offsets[:]))
@@ -104,7 +104,7 @@ def tile_picked_zbloom_none_po_kernel(
         w2_raw = reused.tile([P, PACK, N], F32, name="w2_raw", offset=0)
         nc.sync.dma_start(out=w2_raw[:], in_=w2.rearrange("(p j) c -> p j c", j=PACK))
         x_w = []
-        for lo, hi in ((0, 2), (2, 4)):
+        for lo, hi in ((0, 1), (1, 2), (2, 4)):
             picked = tile([P, (hi - lo) * V], U32, "x_w%d" % lo)
             nc.vector.tensor_copy(picked[:], word_table[:].indirect(offsets[:, lo * 16 : hi * 16]))
             x_w.extend(picked[:, d * V : (d + 1) * V] for d in range(hi - lo))
@@ -157,7 +157,7 @@ def tile_picked_zbloom_none_po_kernel(
                 terms[n][:, :, :, part * Q : (part + 1) * Q],
                 planes(d, part),
                 COPY,
-                scale=gate_last if d == D - 1 else gate_col[:, 0, d : d + 1],
+                scale=gate_last if d == 2 else gate_col[:, 0, d : d + 1],
             )
 
         def joined_term(d, part, u):

@@ -71,12 +71,12 @@ def tile_picked_zbloom_none_po_kernel(
                 out=rounded[:].rearrange("p (u q e j) -> p q j u e", u=2, e=2, j=PACK),
                 in_=w1_raw[part].rearrange("p j (q u e) -> p q j u e", u=2, e=2),
             )
-            return rounded
+            return rounded[:]
 
         def quantise_w1(part, rounded):
             codes = tile([P, HALF], U32, "w1_codes%d" % part)
             scales = tile([P, HALF], U8, "w1_scales%d" % part)
-            nc.vector.quantize_mx(out=codes[:].bitcast(FP8X4), scales=scales[:], in_=rounded[:])
+            nc.vector.quantize_mx(out=codes[:].bitcast(FP8X4), scales=scales[:], in_=rounded)
             return codes, scales
 
         w1_first = round_w1(0)
@@ -101,8 +101,10 @@ def tile_picked_zbloom_none_po_kernel(
         late_raw = reused.tile([P, PACK * HALF + 16], F32, name="w1_raw1", offset=10208)
         late_rows.append(late_raw[:, : 2 * HALF].rearrange("p (j c) -> p j c", j=2))
         nc.sync.dma_start(out=late_rows[1], in_=w1_in[:, 2:, HALF:])
-        w2_raw = reused.tile([P, PACK, N], F32, name="w2_raw", offset=0)
-        nc.sync.dma_start(out=w2_raw[:], in_=w2.rearrange("(p j) c -> p j c", j=PACK))
+        w2_raw = reused.tile([P, 2, PACK, HALF], F32, name="w2_raw", offset=0)
+        for half in range(2):
+            columns = slice(half * HALF, (half + 1) * HALF)
+            nc.sync.dma_start(out=w2_raw[:, half], in_=w2.rearrange("(p j) c -> p j c", j=PACK)[:, :, columns])
         x_w = []
         for lo, hi in ((0, 1), (1, 2), (2, 4)):
             picked = tile([P, (hi - lo) * V], U32, "x_w%d" % lo)
@@ -121,10 +123,10 @@ def tile_picked_zbloom_none_po_kernel(
                 stop=True,
             )
 
-        w1_late = tile([P, HALF * PACK], BF16, "w1_bf1")
+        w1_late = w2_bf[:, : HALF * PACK]
         for n, rows in enumerate(late_rows):
             nc.scalar.copy(
-                out=w1_late[:].rearrange("p (u q e j) -> p q j u e", u=2, e=2, j=PACK)[:, :, 2 * n : 2 * n + 2],
+                out=w1_late.rearrange("p (u q e j) -> p q j u e", u=2, e=2, j=PACK)[:, :, 2 * n : 2 * n + 2],
                 in_=rows.rearrange("p j (q u e) -> p q j u e", u=2, e=2),
             )
         w1_mx.append(quantise_w1(1, w1_late))
@@ -178,7 +180,7 @@ def tile_picked_zbloom_none_po_kernel(
                     ADD,
                 )
                 return
-            nxt = tile([P, HALF], F32, "acc%d%d" % (d, part), {(1, 0): "w1_bf1", (1, 1): "w2_codes"}.get((d, part)))
+            nxt = tile([P, HALF], F32, "acc%d%d" % (d, part), "w2_codes" if (d, part) == (1, 1) else None)
             nc.vector.scalar_tensor_tensor(nxt[:], y[d, 1, part], gate_d, acc[part][:], MULT, ADD)
             acc[part] = nxt
 
@@ -214,11 +216,13 @@ def tile_picked_zbloom_none_po_kernel(
             nc.tensor.transpose(z_pairs[:, u, :], z_rows[:, u, :].bitcast(F32), ident[:])
 
         rounded = w2_bf[:].rearrange("p (t m j) -> p m t j", t=PACK, j=PACK)
-        source = w2_raw[:].rearrange("p j (m t) -> p m t j", t=PACK)
-        own = 88
-        nc.gpsimd.tensor_scalar(rounded[:, :own], source[:, :own], 1.0, 0.0, MULT, ADD)
+        source = [w2_raw[:, half].rearrange("p j (m t) -> p m t j", t=PACK) for half in range(2)]
+        own = Q // 2
+        nc.gpsimd.tensor_scalar(rounded[:, :Q], source[0], 1.0, 0.0, MULT, ADD)
+        nc.gpsimd.tensor_scalar(rounded[:, Q : Q + own], source[1][:, :own], 1.0, 0.0, MULT, ADD)
         nc.scalar.copy(
-            out=rounded[:, own:].rearrange("p m t j -> p m j t"), in_=source[:, own:].rearrange("p m t j -> p m j t")
+            out=rounded[:, Q + own :].rearrange("p m t j -> p m j t"),
+            in_=source[1][:, own:].rearrange("p m t j -> p m j t"),
         )
         w2_codes = tile([P, N], U32, "w2_codes")
         w2_scales = tile([P, N], U8, "w2_scales")

@@ -59,8 +59,8 @@ def tile_picked_zbloom_none_po_kernel(
         nc.sync.dma_start(out=word_table[:, :first].bitcast(I32), in_=words_in[:, :first])
         nc.sync.dma_start(out=gate_rows[0:D, :], in_=gate[:, 0, :])
         nc.sync.dma_start(out=word_table[:, first:].bitcast(I32), in_=words_in[:, first:])
-        late_rows = [tile([P, 2, HALF], F32, "w1_late0")[:]]
-        nc.sync.dma_start(out=late_rows[0], in_=w1_in[:, :2, HALF:])
+        late_rows = [tile([P, PACK, P], F32, "w1_late0")[:]]
+        nc.sync.dma_start(out=late_rows[0], in_=w1_in[:, :, HALF : HALF + P])
 
         ident = tile([P, P], F32, "ident")
         make_identity(nc, ident[:])
@@ -99,8 +99,8 @@ def tile_picked_zbloom_none_po_kernel(
         for j in range(1, 4):
             nc.sync.dma_start(out=x_sc[j:P:32, :].bitcast(I32), in_=picked_sc[8 * j : P : 32, :].bitcast(I32))
         late_raw = reused.tile([P, PACK * HALF + 16], F32, name="w1_raw1", offset=10208)
-        late_rows.append(late_raw[:, : 2 * HALF].rearrange("p (j c) -> p j c", j=2))
-        nc.sync.dma_start(out=late_rows[1], in_=w1_in[:, 2:, HALF:])
+        late_rows.append(late_raw[:, : 2 * HALF].rearrange("p (j c) -> p j c", j=PACK))
+        nc.sync.dma_start(out=late_rows[1], in_=w1_in[:, :, HALF + P :])
         w2_raw = reused.tile([P, 2, PACK, HALF], F32, name="w2_raw", offset=0)
         for half in range(2):
             columns = slice(half * HALF, (half + 1) * HALF)
@@ -126,7 +126,7 @@ def tile_picked_zbloom_none_po_kernel(
         w1_late = w2_bf[:, : HALF * PACK]
         for n, rows in enumerate(late_rows):
             nc.scalar.copy(
-                out=w1_late.rearrange("p (u q e j) -> p q j u e", u=2, e=2, j=PACK)[:, :, 2 * n : 2 * n + 2],
+                out=w1_late.rearrange("p (u q e j) -> p q j u e", u=2, e=2, j=PACK)[:, n * (Q // 2) : (n + 1) * (Q // 2)],
                 in_=rows.rearrange("p j (q u e) -> p q j u e", u=2, e=2),
             )
         w1_mx.append(quantise_w1(1, w1_late))

@@ -42,10 +42,9 @@ def tile_picked_zbloom_none_po_kernel(
             return sb.tile(shape, dtype, name=name, tag=tag or name, align_bytes=64)
 
         scale_table = reused.tile([P, T], U8, name="scale_table", offset=6144)
-        nc.gpsimd.memset(scale_table[:, : T // 2].bitcast(I32), 0)
-        nc.vector.memset(scale_table[:, T // 2 :].bitcast(I32), 0)
+        nc.vector.memset(scale_table[:].bitcast(I32), 0)
         gate_rows = tile([P, V], F32, "gate_rows")
-        nc.gpsimd.memset(gate_rows[:], 0.0)
+        nc.vector.memset(gate_rows[:], 0.0)
 
         w1_in = w1.rearrange("(p j) c -> p j c", j=PACK)
         w1_raw = [tile([P, PACK, HALF], F32, "w1_raw0")[:]]
@@ -63,7 +62,8 @@ def tile_picked_zbloom_none_po_kernel(
         nc.sync.dma_start(out=late_rows[0], in_=w1_in[:, :, HALF : HALF + P])
 
         ident = tile([P, P], F32, "ident")
-        make_identity(nc, ident[:])
+        nc.vector.memset(ident[:], 0.0)
+        make_identity(nc, ident[:], nomemset=True)
 
         def round_w1(part):
             rounded = tile([P, HALF * PACK], BF16, "w1_bf%d" % part)

@@ -162,10 +162,10 @@ def tile_picked_zbloom_none_po_kernel(
                 scale=gate_last if d == 2 else gate_col[:, 0, d : d + 1],
             )
 
-        def joined_term(d, part, u):
+        def joined_term(n, d, part, u):
             places = slice(part * Q, (part + 1) * Q)
             nc.vector.scalar_tensor_tensor(
-                terms[3][:, u, :, places], planes(d, part)[:, u], gate_col[:, 0, d : d + 1], terms[0][:, u, :, places], MULT, ADD
+                terms[n][:, u, :, places], planes(d, part)[:, u], gate_col[:, 0, d : d + 1], terms[0][:, u, :, places], MULT, ADD
             )
 
         def chain(d, part):
@@ -191,14 +191,14 @@ def tile_picked_zbloom_none_po_kernel(
         seeds = (reused.tile([P, HALF], F32, name="seed0", offset=9216), tile([P, HALF], F32, "seed1"))
         for part in range(2):
             seed(part, seeds[part])
-            for n, d in ((0, 0), (1, 2), (2, 3)):
+            for n, d in (((0, 0), (1, 2), (2, 3)), ((3, 0), (0, 2), (2, 3)))[part]:
                 own_term(n, d, part)
             chain(1, part)
             for u in range(2):
-                joined_term(1, part, u)
+                joined_term((3, 1)[part], 1, part, u)
             chain(2, part)
             chain(3, part)
-        terms = (terms[1], terms[3], terms[2])
+        terms = (terms[3], terms[2], terms[1])
 
         z_sum = bank(0, [P, PACK, P], "z_sum")
         for n, term in enumerate(terms):

@@ -217,7 +217,7 @@ def tile_picked_zbloom_none_po_kernel(
 
         rounded = w2_bf[:].rearrange("p (t m j) -> p m t j", t=PACK, j=PACK)
         source = [w2_raw[:, half].rearrange("p j (m t) -> p m t j", t=PACK) for half in range(2)]
-        own = Q // 2
+        own = Q // 4
         nc.gpsimd.tensor_scalar(rounded[:, :Q], source[0], 1.0, 0.0, MULT, ADD)
         nc.gpsimd.tensor_scalar(rounded[:, Q : Q + own], source[1][:, :own], 1.0, 0.0, MULT, ADD)
         nc.scalar.copy(

from contextlib import ExitStack

import concourse.mybir as mybir
from concourse.masks import make_identity

K, T, S, D, V, H, N = 512, 4096, 1024, 4, 256, 512, 512
P = 128
PACK = 4
HALVES = V // P
HALF = 256
Q = HALF // PACK

FLOPS = 2 * K * H * S + 2 * H * N * V
BYTES = P * T * PACK + 16 * T + 4 * K * H + 4 * H * N + 4 * D * V + 2 * P * S // 16 + 4 * N * V + N * V + 16 * V

F32 = mybir.dt.float32
BF16 = mybir.dt.bfloat16
I32 = mybir.dt.int32
U32 = mybir.dt.uint32
U16 = mybir.dt.uint16
U8 = mybir.dt.uint8
FP8X4 = mybir.dt.float8_e4m3fn_x4
MULT = mybir.AluOpType.mult
ADD = mybir.AluOpType.add
COPY = mybir.ActivationFunctionType.Copy


def tile_picked_zbloom_none_po_kernel(
    tc, x_words, x_scales, w1, w2, gate, offs, out_0, out_1, out_2
):
    nc = tc.nc
    with ExitStack() as ctx:
        sb = ctx.enter_context(tc.tile_pool(name="sb", bufs=1))
        ps = ctx.enter_context(tc.psum_pool(name="ps", bufs=1))

        reused = ctx.enter_context(tc.tile_pool(name="reused", bufs=1))

        def bank(b, shape, name):
            return ps.tile(shape, F32, name=name, tag="bank%d" % b)

        def tile(shape, dtype, name, tag=None):
            return sb.tile(shape, dtype, name=name, tag=tag or name, align_bytes=64)

        scale_table = reused.tile([P, T], U8, name="scale_table", offset=6144)
        nc.vector.memset(scale_table[:].bitcast(I32), 0)
        gate_rows = tile([P, V], F32, "gate_rows")
        nc.vector.memset(gate_rows[:], 0.0)

        w1_in = w1.rearrange("(p j) c -> p j c", j=PACK)
        w1_raw = [tile([P, PACK, HALF], F32, "w1_raw0")[:]]
        nc.sync.dma_start(out=w1_raw[0], in_=w1_in[:, :, :HALF])
        offsets = sb.tile([P, S // 16], U16, name="offsets")
        nc.sync.dma_start(offsets[:], offs)
        nc.sync.dma_start(out=scale_table[0:P:8, :].bitcast(I32), in_=x_scales[0].bitcast(I32))
        word_table = tile([P, T], U32, "word_table")
        words_in = x_words[0].rearrange("p n t -> p (n t)").bitcast(I32)
        first = 3 * T // 4
        nc.sync.dma_start(out=word_table[:, :first].bitcast(I32), in_=words_in[:, :first])
        nc.sync.dma_start(out=gate_rows[0:D, :], in_=gate[:, 0, :])
        nc.sync.dma_start(out=word_table[:, first:].bitcast(I32), in_=words_in[:, first:])
        late_rows = [tile([P, PACK, P], F32, "w1_late0")[:]]
        nc.sync.dma_start(out=late_rows[0], in_=w1_in[:, :, HALF : HALF + P])

        ident = tile([P, P], F32, "ident")
        nc.vector.memset(ident[:], 0.0)
        make_identity(nc, ident[:], nomemset=True)

        def round_w1(part):
            rounded = tile([P, HALF * PACK], BF16, "w1_bf%d" % part)
            nc.scalar.copy(
                out=rounded[:].rearrange("p (u q e j) -> p q j u e", u=2, e=2, j=PACK),
                in_=w1_raw[part].rearrange("p j (q u e) -> p q j u e", u=2, e=2),
            )
            return rounded[:]

        def quantise_w1(part, rounded):
            codes = tile([P, HALF], U32, "w1_codes%d" % part)
            scales = tile([P, HALF], U8, "w1_scales%d" % part)
            nc.vector.quantize_mx(out=codes[:].bitcast(FP8X4), scales=scales[:], in_=rounded)
            return codes, scales

        w1_first = round_w1(0)

        gate_ps = bank(7, [P, HALVES, P], "gate_ps")
        for h in range(HALVES):
            nc.tensor.transpose(gate_ps[:, h, :], gate_rows[:, h * P : (h + 1) * P], ident[:])
        gate_col = tile([P, HALVES, D], F32, "gate_col")
        nc.scalar.activation(gate_col[:], gate_ps[:, :, 0:D], COPY)

        w2_bf = tile([P, N * PACK], BF16, "w2_bf")
        gate_last = w2_bf[:, N * PACK - 2 :].bitcast(F32)
        nc.scalar.activation(gate_last, gate_ps[:, 0, 2:3], COPY)

        picked_sc = tile([P, S], U8, "picked_sc")
        nc.vector.tensor_copy(picked_sc[:], scale_table[:].indirect(offsets[:]))
        w1_mx = [quantise_w1(0, w1_first)]
        x_sc = tile([P, S], U8, "x_sc")
        nc.vector.tensor_copy(x_sc[:].bitcast(I32), picked_sc[:].bitcast(I32))
        for j in range(1, 4):
            nc.sync.dma_start(out=x_sc[j:P:32, :].bitcast(I32), in_=picked_sc[8 * j : P : 32, :].bitcast(I32))
        late_raw = reused.tile([P, PACK * HALF + 16], F32, name="w1_raw1", offset=10208)
        late_rows.append(late_raw[:, : 2 * HALF].rearrange("p (j c) -> p j c", j=PACK))
        nc.sync.dma_start(out=late_rows[1], in_=w1_in[:, :, HALF + P :])
        w2_raw = reused.tile([P, 2, PACK, HALF], F32, name="w2_raw", offset=0)
        for half in range(2):
            columns = slice(half * HALF, (half + 1) * HALF)
            nc.sync.dma_start(out=w2_raw[:, half], in_=w2.rearrange("(p j) c -> p j c", j=PACK)[:, :, columns])
        x_w = []
        for lo, hi in ((0, 1), (1, 2), (2, 4)):
            picked = tile([P, (hi - lo) * V], U32, "x_w%d" % lo)
            nc.vector.tensor_copy(picked[:], word_table[:].indirect(offsets[:, lo * 16 : hi * 16]))
            x_w.extend(picked[:, d * V : (d + 1) * V] for d in range(hi - lo))

        warm = bank(7, [P, HALF], "warm")
        for turn in range(2):
            nc.tensor.matmul_mx(
                out=warm[:],
                lhsT=w1_mx[0][0][:, :P].bitcast(FP8X4),
                lhsT_scale=w1_mx[0][1][:, :P],
                rhs=w1_mx[0][0][:].bitcast(FP8X4),
                rhs_scale=w1_mx[0][1][:],
                start=True,
                stop=True,
            )

        w1_late = w2_bf[:, : HALF * PACK]
        for n, rows in enumerate(late_rows):
            nc.scalar.copy(
                out=w1_late.rearrange("p (u q e j) -> p q j u e", u=2, e=2, j=PACK)[:, n * (Q // 2) : (n + 1) * (Q // 2)],
                in_=rows.rearrange("p j (q u e) -> p q j u e", u=2, e=2),
            )
        w1_mx.append(quantise_w1(1, w1_late))

        y = {}
        shares = (((0, 1), (0, 0)), ((1, 1), (1, 0)), ((2, 0), (3, 0)), ((2, 1), (3, 1)))
        for part, (n, pieces) in ((part, share) for part in range(2) for share in enumerate(shares)):
            held = bank(4 * part + n, [P, 2, HALF], "y%d%d" % (part, n))
            for e, (d, h) in enumerate(pieces):
                y[d, h, part] = held[:, e, :]
                nc.tensor.matmul_mx(
                    out=y[d, h, part],
                    lhsT=x_w[d][:, h * P : (h + 1) * P].bitcast(FP8X4),
                    lhsT_scale=x_sc[:, d * V + h * P : d * V + (h + 1) * P],
                    rhs=w1_mx[part][0][:].bitcast(FP8X4),
                    rhs_scale=w1_mx[part][1][:],
                    start=True,
                    stop=True,
                )

        terms = [reused.tile([P, 2, 2, P], F32, name="term%d" % d, offset=10240 + d * H * 4) for d in range(D)]
        z_rows = tile([P, 2, HALF], BF16, "z_rows")
        acc = {}

        def planes(d, part):
            return y[d, 0, part].rearrange("p (u q e) -> p u e q", u=2, e=2)

        def own_term(n, d, part):
            nc.scalar.activation(
                terms[n][:, :, :, part * Q : (part + 1) * Q],
                planes(d, part),
                COPY,
                scale=gate_last if d == 2 else gate_col[:, 0, d : d + 1],
            )

        def joined_term(n, d, part, u):
            places = slice(part * Q, (part + 1) * Q)
            nc.vector.scalar_tensor_tensor(
                terms[n][:, u, :, places], planes(d, part)[:, u], gate_col[:, 0, d : d + 1], terms[0][:, u, :, places], MULT, ADD
            )

        def chain(d, part):
            gate_d = gate_col[:, 1, d : d + 1]
            if d == D - 1:
                nc.vector.scalar_tensor_tensor(
                    z_rows[:, :, part * P : (part + 1) * P],
                    y[d, 1, part].rearrange("p (u c) -> p u c", u=2),
                    gate_d,
                    acc[part][:].rearrange("p (u c) -> p u c", u=2),
                    MULT,
                    ADD,
                )
                return
            nxt = tile([P, HALF], F32, "acc%d%d" % (d, part), "w2_codes" if (d, part) == (1, 1) else None)
            nc.vector.scalar_tensor_tensor(nxt[:], y[d, 1, part], gate_d, acc[part][:], MULT, ADD)
            acc[part] = nxt

        def seed(part, into):
            acc[part] = into
            nc.scalar.activation(into[:], y[0, 1, part], COPY, scale=gate_col[:, 1, 0:1])

        seeds = (reused.tile([P, HALF], F32, name="seed0", offset=9216), tile([P, HALF], F32, "seed1"))
        for part in range(2):
            seed(part, seeds[part])
            for n, d in (((0, 0), (1, 2), (2, 3)), ((3, 0), (0, 2), (2, 3)))[part]:
                own_term(n, d, part)
            chain(1, part)
            for u in range(2):
                joined_term((3, 1)[part], 1, part, u)
            chain(2, part)
            chain(3, part)
        terms = (terms[3], terms[2], terms[1])

        z_sum = bank(0, [P, PACK, P], "z_sum")
        for n, term in enumerate(terms):
            for t in range(PACK):
                nc.tensor.matmul(
                    z_sum[:, t, :],
                    lhsT=term[:, t // 2, t % 2, :],
                    rhs=ident[:],
                    is_transpose=True,
                    start=(n == 0 and t == 0),
                    stop=(n == len(terms) - 1 and t == PACK - 1),
                )
        z_pairs = bank(6, [P, 2, P], "z_pairs")
        for u in range(2):
            nc.tensor.transpose(z_pairs[:, u, :], z_rows[:, u, :].bitcast(F32), ident[:])

        rounded = w2_bf[:].rearrange("p (t m j) -> p m t j", t=PACK, j=PACK)
        source = [w2_raw[:, half].rearrange("p j (m t) -> p m t j", t=PACK) for half in range(2)]
        own = Q // 4
        nc.gpsimd.tensor_scalar(rounded[:, :Q], source[0], 1.0, 0.0, MULT, ADD)
        nc.gpsimd.tensor_scalar(rounded[:, Q : Q + own], source[1][:, :own], 1.0, 0.0, MULT, ADD)
        nc.scalar.copy(
            out=rounded[:, Q + own :].rearrange("p m t j -> p m j t"),
            in_=source[1][:, own:].rearrange("p m t j -> p m j t"),
        )
        w2_codes = tile([P, N], U32, "w2_codes")
        w2_scales = tile([P, N], U8, "w2_scales")
        nc.vector.quantize_mx(out=w2_codes[:].bitcast(FP8X4), scales=w2_scales[:], in_=w2_bf[:])

        z_codes = tile([P, V], U32, "z_codes")
        z_scales = tile([P, V], U8, "z_scales")
        for h in range(HALVES):
            cols = slice(h * P, (h + 1) * P)
            z_bf = tile([P, P * PACK], BF16, "z_bf%d" % h)
            if h == 0:
                nc.scalar.copy(
                    out=z_bf[:].rearrange("p (v t) -> p v t", t=PACK),
                    in_=z_sum[:].rearrange("p t v -> p v t"),
                )
            else:
                nc.scalar.copy(
                    out=z_bf[:].bitcast(F32).rearrange("p (v u) -> p v u", u=2),
                    in_=z_pairs[:].rearrange("p u v -> p v u"),
                )
            nc.vector.quantize_mx(out=z_codes[:, cols].bitcast(FP8X4), scales=z_scales[:, cols], in_=z_bf[:])

        out_codes = tile([P, V], U32, "out_codes")
        out_scales = tile([P, V], U8, "out_scales")
        out_view = out_0.rearrange("(p t) v -> p t v", t=PACK)
        o_f32 = tile([P, PACK, V], F32, "o_f32")
        for h in range(HALVES):
            cols = slice(h * P, (h + 1) * P)
            for pair in range(2):
                o_ps = bank(1 + 2 * h + pair, [P, 2, P], "o_ps%d%d" % (h, pair))
                for e in range(2):
                    nc.tensor.matmul_mx(
                        out=o_ps[:, e, :],
                        lhsT=w2_codes[:, (2 * pair + e) * P : (2 * pair + e + 1) * P].bitcast(FP8X4),
                        lhsT_scale=w2_scales[:, (2 * pair + e) * P : (2 * pair + e + 1) * P],
                        rhs=z_codes[:, cols].bitcast(FP8X4),
                        rhs_scale=z_scales[:, cols],
                        start=True,
                        stop=True,
                    )
                copy = nc.vector.tensor_copy if (h, pair) == (0, 1) else nc.scalar.copy
                rows = slice(2 * pair, 2 * pair + 2)
                copy(out=o_f32[:, rows, cols], in_=o_ps[:])
                if h == HALVES - 1:
                    nc.sync.dma_start(out=out_view[:, rows, :], in_=o_f32[:, rows, :])
            o_bf = tile([P, P * PACK], BF16, "o_bf%d" % h)
            own = (P // 4, 20)[h]
            for copy, lo, hi in ((nc.vector.tensor_copy, 0, own), (nc.scalar.copy, own, P // 4))[: h + 1]:
                copy(
                    out=o_bf[:].rearrange("p (c i t) -> p c t i", t=PACK, i=4)[:, lo:hi],
                    in_=o_f32[:, :, cols].rearrange("p t (c i) -> p c t i", i=4)[:, lo:hi],
                )
            nc.vector.quantize_mx(out=out_codes[:, cols].bitcast(FP8X4), scales=out_scales[:, cols], in_=o_bf[:])
            nc.scalar.dma_start(
                out=out_1[0].rearrange("p n t -> p (n t)").bitcast(I32)[:, cols],
                in_=out_codes[:, cols].bitcast(I32),
            )
        for q in range(4):
            queue = nc.sync if q < 3 else nc.scalar
            queue.dma_start(
                out=out_2[0, 4 * q : 4 * q + 4, :].bitcast(I32),
                in_=out_scales[32 * q : 32 * q + 4, :].bitcast(I32),
            )
